import numpy as np
import ml_dtypes


def mxq(x, axis, fmt="e4m3"):
    dtype, down = {"e4m3": (ml_dtypes.float8_e4m3fn, 7), "e5m2": (ml_dtypes.float8_e5m2, 14)}[fmt]
    v = np.moveaxis(np.asarray(x, np.float32).astype(ml_dtypes.bfloat16).astype(np.float64), axis, -1)
    blocks = v.reshape(v.shape[:-1] + (-1, 32))
    amax = np.abs(blocks).max(-1, keepdims=True)
    byte = np.maximum(np.where(amax > 0, np.frexp(amax)[1] - 1 + 127, 0) - down, 1)
    scale = np.exp2(byte - 127.0)
    codes = (blocks / scale).astype(np.float32).astype(dtype).astype(np.float64)
    return np.moveaxis((codes * scale).reshape(v.shape), -1, axis)


WIDE = False


def mx_kscale(k):
    if not WIDE:
        return np.ones(k)
    levels = np.array([10, -10, 5, -5, 0])
    if k % 512:
        return np.exp2(np.random.permutation(np.resize(levels, k // 32))).repeat(32)
    a = np.empty((k // 512, 16))
    for p in range(k // 512):
        a[p, :8] = np.random.permutation(np.resize(levels, 8))
        for g in range(8):
            far = levels[np.abs(levels - a[p, g]) >= 10]
            a[p, g + 8] = far[np.random.randint(len(far))]
    return np.exp2(a.ravel()).repeat(32)


def f64(x):
    return np.asarray(x).astype(np.float64)


def striped(idx):
    return np.tile(idx.reshape(-1, 16).T, (8, 1)).astype(np.uint16)


def unstriped(offs):
    return offs[:16].T.reshape(-1).astype(np.int64)


E2M1 = np.array([0.0, 0.5, 1.0, 1.5, 2.0, 3.0, 4.0, 6.0, -0.0, -0.5, -1.0, -1.5, -2.0, -3.0, -4.0, -6.0])


def pack_weight(w, fmt):
    k, n = w.shape
    w = f64(np.asarray(w, np.float32).astype(ml_dtypes.bfloat16)).reshape(k // 32, 32, n)
    amax = np.abs(w).max(1)
    if fmt == "e4m3":
        byte = np.frexp(amax)[1] - 1 + 127 - 7
    else:
        mant, ex = np.frexp(amax / 6.0)
        byte = np.where(mant > 0.5, ex, ex - 1) + 127
    byte = np.clip(np.where(amax > 0, byte, 1), 1, 254)
    scaled = (w * np.exp2(127.0 - byte)[:, None, :]).reshape(k, n).astype(np.float32)
    by_word = np.ascontiguousarray(scaled.reshape(k // 512, 128, 4, n).transpose(0, 1, 3, 2))
    if fmt == "e4m3":
        words = by_word.astype(ml_dtypes.float8_e4m3fn).view(np.uint8)
    else:
        c = by_word.astype(ml_dtypes.float4_e2m1fn).view(np.uint8) & 0xF
        words = (c[..., 0::2] | (c[..., 1::2] << 4)).reshape(k // 512, 128, 2 * n)
    return np.ascontiguousarray(words), np.ascontiguousarray(byte.astype(np.uint8).reshape(k // 512, 16, n))


def unpack_weight(words, scales, fmt):
    g, _, n = scales.shape
    words = np.ascontiguousarray(words).reshape(g, 128, n, -1)
    if fmt == "e4m3":
        vals = words.view(ml_dtypes.float8_e4m3fn).astype(np.float64)
    else:
        nib = np.empty((g, 128, n, 4), np.uint8)
        nib[..., 0::2] = words & 0xF
        nib[..., 1::2] = words >> 4
        vals = E2M1[nib]
    vals = vals * np.repeat(np.exp2(scales.astype(np.float64) - 127.0), 8, axis=1)[..., None]
    return vals.transpose(0, 1, 3, 2).reshape(g * 512, n)


def gelu(v):
    return 0.5 * v * (1.0 + np.tanh(np.sqrt(2.0 / np.pi) * (v + 0.044715 * v**3)))


def often(T, S):
    return np.random.permutation(T)[(T * np.random.uniform(0, 1, S) ** 4).astype(np.int64)]


def bf(x):
    return np.asarray(x, np.float32).astype(ml_dtypes.bfloat16)


def planes(Y):
    n, m = Y.shape
    b = f64(bf(Y)).reshape(n // 32, 32, m)
    amax = np.abs(b).max(1)
    byte = np.clip(np.where(amax > 0, np.frexp(amax)[1] - 1 + 127 - 7, 1), 1, 254)
    codes = (b * np.exp2(127.0 - byte)[:, None, :]).reshape(n, m).astype(np.float32).astype(ml_dtypes.float8_e4m3fn).view(np.uint8)
    words = codes.reshape(n // 512, 128, 4, m).transpose(0, 1, 3, 2)
    return np.ascontiguousarray(words), np.ascontiguousarray(byte.astype(np.uint8).reshape(n // 512, 16, m))


K, K2, T, T2, S, H, N = 1024, 512, 1024, 2048, 512, 1024, 512

def setup_inputs():
    n = np.random.standard_normal
    s, s2, u = mx_kscale(K)[:, None], mx_kscale(K2)[:, None], mx_kscale(H)[:, None]
    size = np.exp(0.8 * n((1, N)))
    tab_words, tab_scales = pack_weight(n((K, T)) * s, "e4m3")
    tab2_words, tab2_scales = pack_weight(n((K2, T2)) * s2, "e2m1")
    w1_words, w1_scales = pack_weight(0.45 * n((K, H)) / np.sqrt(K) / s, "e2m1")
    w3_words, w3_scales = pack_weight(n((H, N)) / np.sqrt(H) * size / u, "e4m3")
    return {
        "tab_words": tab_words, "tab_scales": tab_scales,
        "tab2_words": tab2_words, "tab2_scales": tab2_scales,
        "offs": striped(often(T, S)), "offs2": striped(often(T2, S)),
        "w1_words": w1_words, "w1_scales": w1_scales,
        "w2": (0.3 * n((K2, H)) / np.sqrt(K2) / s2).astype(np.float32),
        "w3_words": w3_words, "w3_scales": w3_scales,
        "w4": (n((H, N)) / np.sqrt(H) * size / u).astype(np.float32),
        "gl": (np.random.uniform(1.0, 3.0, H) * u[:, 0]).astype(np.float32),
        "gs": (np.random.uniform(1.0, 3.0, H) * u[:, 0]).astype(np.float32),
    }

def reference(tab_words, tab_scales, tab2_words, tab2_scales, offs, offs2,
              w1_words, w1_scales, w2, w3_words, w3_scales, w4, gl, gs):
    v = unpack_weight(tab_words, tab_scales, "e4m3")[:, unstriped(offs)]
    v2 = unpack_weight(tab2_words, tab2_scales, "e2m1")[:, unstriped(offs2)]
    w1 = unpack_weight(w1_words, w1_scales, "e2m1")
    w3 = unpack_weight(w3_words, w3_scales, "e4m3")
    a = w1.T @ v
    load = mxq(f64(w2), 0, "e4m3").T @ v2
    gated = a / (1.0 + np.exp(-a))
    z = np.sin(gated - load) * f64(gs)[:, None]
    x = load * f64(gl)[:, None]
    xq = mxq(x, 0, "e4m3")
    zq = mxq(z, 0, "e4m3")
    y = w3.T @ xq + mxq(f64(w4), 0, "e4m3").T @ zq
    words, scales = planes(y)
    return y, words, scales

@@ -1,0 +1,297 @@
+from contextlib import ExitStack
+
+import concourse.mybir as mybir
+
+K, K2, T, T2, S, H, N = 1024, 512, 1024, 2048, 512, 1024, 512
+FLOPS = 2 * S * H * (K + K2 + 2 * N)
+
+F32 = mybir.dt.float32
+BF16 = mybir.dt.bfloat16
+I32 = mybir.dt.int32
+U32 = mybir.dt.uint32
+U16 = mybir.dt.uint16
+U8 = mybir.dt.uint8
+FP8X4 = mybir.dt.float8_e4m3fn_x4
+FP4X4 = mybir.dt.float4_e2m1fn_x4
+ACT = mybir.ActivationFunctionType
+ALU = mybir.AluOpType
+
+P = 128
+PACK = 4
+PASS = P * PACK
+QUADS = 4
+JB = 128
+HALF = 256
+
+
+def tile_list_forklift_tipping_features_kernel(
+    tc, tab_words, tab_scales, tab2_words, tab2_scales, offs, offs2,
+    w1_words, w1_scales, w2, w3_words, w3_scales, w4, gl, gs, out_0, out_1, out_2,
+):
+    nc = tc.nc
+    with ExitStack() as ctx:
+        keep = ctx.enter_context(tc.tile_pool(name="keep", bufs=1))
+        work = ctx.enter_context(tc.tile_pool(name="work", bufs=3))
+        psum1 = ctx.enter_context(tc.psum_pool(name="psum1", bufs=2))
+        psum2 = ctx.enter_context(tc.psum_pool(name="psum2", bufs=1))
+
+        def held(name, cols, dtype):
+            return keep.tile([P, cols], dtype, name=name, align_bytes=64)
+
+        idx = keep.tile([P, S // 16], U16, name="idx")
+        idx2 = keep.tile([P, S // 16], U16, name="idx2")
+        tab_sc = held("tab_sc", 2 * T, U8)
+        tab2_sc = held("tab2_sc", T2, U8)
+        w1_sc = held("w1_sc", 2 * H, U8)
+        w3_sc = held("w3_sc", N, U8)
+        tab_w = [held("tab_w%d" % a, T, U32) for a in range(2)]
+        tab2_w = held("tab2_w", T2, U16)
+        w1_w = [held("w1_w%d" % b, 2 * PASS, U16) for b in range(2)]
+        w3_w = held("w3_w", 2 * N, U32)
+        w2_raw = [held("w2_raw%d" % b, PACK * PASS, F32) for b in range(2)]
+        w4_raw = [held("w4_raw%d" % b, PACK * N, F32) for b in range(2)]
+        gl_sb = held("gl_sb", 2 * PACK, F32)
+        gs_sb = held("gs_sb", 2 * PACK, F32)
+
+        nc.vector.memset(tab2_sc[:].bitcast(I32), 0)
+        nc.vector.memset(tab_sc[:].bitcast(I32), 0)
+        warm = held("warm", 16, F32)
+        nc.gpsimd.memset(warm[:, 0:1], 0.0)
+        nc.gpsimd.memset(w1_sc[:].bitcast(I32), 0)
+        nc.scalar.activation(out=warm[:, 8:9], in_=warm[:, 0:1], func=ACT.Silu)
+
+        def load_scale_rows(queue, dst, src):
+            for q in range(QUADS):
+                queue.dma_start(
+                    out=dst[32 * q : 32 * q + 4, :].bitcast(I32).rearrange("r (a n) -> r a n", a=src.shape[0]),
+                    in_=src[:, 4 * q : 4 * q + 4, :].bitcast(I32).rearrange("a r n -> r a n"),
+                )
+
+        def load_rows(dst, src):
+            nc.sync.dma_start(
+                out=dst[:].rearrange("p (i c) -> p i c", i=PACK),
+                in_=src.rearrange("(p i) c -> p i c", i=PACK),
+            )
+
+        def load_w1_words(b):
+            nc.sync.dma_start(
+                out=w1_w[b][:].bitcast(I32).rearrange("p (a n) -> p a n", a=2),
+                in_=w1_words[:, :, 2 * PASS * b : 2 * PASS * (b + 1)].bitcast(I32).rearrange("a p n -> p a n"),
+            )
+
+        def load_tab_words(a):
+            nc.sync.dma_start(
+                out=tab_w[a][:].bitcast(I32), in_=tab_words[a].rearrange("p n i -> p (n i)").bitcast(I32))
+
+        load_scale_rows(nc.gpsimd, w1_sc, w1_scales)
+        nc.gpsimd.memset(w3_sc[:].bitcast(I32), 0)
+        for q in range(QUADS):
+            nc.gpsimd.dma_start(
+                out=w3_sc[32 * q : 32 * q + 8, :].bitcast(I32),
+                in_=w3_scales[:, 4 * q : 4 * q + 4, :].bitcast(I32),
+            )
+        nc.sync.dma_start(out=tab2_w[:].bitcast(I32), in_=tab2_words[0].bitcast(I32))
+        nc.sync.dma_start(idx2[:], offs2)
+        nc.sync.dma_start(idx[:], offs)
+        load_tab_words(0)
+        load_scale_rows(nc.sync, tab2_sc, tab2_scales)
+        load_rows(w2_raw[0], w2[:, 0:PASS])
+        load_scale_rows(nc.sync, tab_sc, tab_scales)
+        load_tab_words(1)
+        load_w1_words(0)
+        load_w1_words(1)
+        nc.sync.dma_start(
+            out=gl_sb[:].rearrange("p (b t) -> p b t", b=2), in_=gl.rearrange("(b p t) -> p b t", b=2, t=PACK))
+        nc.sync.dma_start(
+            out=gs_sb[:].rearrange("p (b t) -> p b t", b=2), in_=gs.rearrange("(b p t) -> p b t", b=2, t=PACK))
+        load_rows(w2_raw[1], w2[:, PASS : 2 * PASS])
+        nc.sync.dma_start(
+            out=w3_w[:].bitcast(I32).rearrange("p (a n) -> p a n", a=2),
+            in_=w3_words.rearrange("a p n i -> a p (n i)").bitcast(I32).rearrange("a p n -> p a n"),
+        )
+        for b in range(2):
+            load_rows(w4_raw[b], w4[PASS * b : PASS * (b + 1), :])
+
+        def gather(name, dtype, window, offsets, h):
+            picked = held("%s_%d" % (name, h), HALF, dtype)
+            cols = HALF // 16
+            nc.vector.tensor_copy(picked[:], window.indirect(offsets[:, cols * h : cols * (h + 1)]))
+            return picked
+
+        def round_and_deal(name, raw):
+            dealt = held(name + "_bf", PACK * PASS, BF16)
+            nc.scalar.copy(
+                out=dealt[:].rearrange("p (t m i) -> p m t i", t=PACK, i=PACK),
+                in_=raw[:].rearrange("p (i m t) -> p m t i", i=PACK, t=PACK),
+            )
+            return dealt
+
+        def quantise(name, values, cols):
+            codes = held(name + "_codes", cols, U32)
+            scales = held(name + "_scales", cols, U8)
+            nc.vector.quantize_mx(out=codes[:].bitcast(FP8X4), scales=scales[:], in_=values[:])
+            return codes, scales
+
+        def deal(name, dtype, src, run):
+            passes = src.shape[1]
+            dealt = held(name, passes * PASS, dtype)
+            nc.vector.tensor_copy(
+                out=dealt[:].rearrange("p (a t c i) -> p a c t i", a=passes, t=PACK, i=run),
+                in_=src.rearrange("p a (c i t) -> p a c t i", t=PACK, i=run),
+            )
+            return dealt
+
+        v_sc, v_w, v2_sc, v2_w = {}, {}, {}, {}
+        w2_bf = [round_and_deal("w2_%d" % b, w2_raw[b]) for b in range(1)]
+        def deal_w1_scales(b):
+            return deal("w1_sc_dealt%d" % b, U8,
+                        w1_sc[:].rearrange("p (a n) -> p a n", a=2)[:, :, PASS * b : PASS * (b + 1)], 16)
+
+        def deal_w1_words(b):
+            return deal("w1_w_dealt%d" % b, U16, w1_w[b][:].rearrange("p (a n) -> p a n", a=2), 8)
+
+        for h in range(2):
+            v2_w[h] = gather("v2_w", U16, tab2_w[:], idx2, h)
+        for h in range(2):
+            v_w[0, h] = gather("v_w0", U32, tab_w[0][:], idx, h)
+        for h in range(2):
+            v2_sc[h] = gather("v2_sc", U8, tab2_sc[:], idx2, h)
+        w1_sc_d = [deal_w1_scales(b) for b in range(2)]
+        for a in range(2):
+            v_sc[a, 0] = gather("v_sc%d" % a, U8, tab_sc[:, T * a : T * (a + 1)], idx, 0)
+        v_w[1, 0] = gather("v_w1", U32, tab_w[1][:], idx, 0)
+        w1_w_d = [deal_w1_words(0)]
+        w2_q = [quantise("w2_0", w2_bf[0], PASS)]
+        for a in range(2):
+            v_sc[a, 1] = gather("v_sc%d" % a, U8, tab_sc[:, T * a : T * (a + 1)], idx, 1)
+        v_w[1, 1] = gather("v_w1", U32, tab_w[1][:], idx, 1)
+        w1_w_d.append(deal_w1_words(1))
+
+        xz_q = {}
+
+        def first_stage(b, jb):
+            h, j0 = divmod(jb * JB, HALF)
+            js = slice(j0, j0 + JB)
+            l_bank = psum1.tile([P, PASS], F32, name="l_bank")
+            a_bank = psum1.tile([P, PASS], F32, name="a_bank")
+            w1_codes, w1_planes = w1_w_d[b], w1_sc_d[b]
+            for t in range(PACK):
+                for a in range(2):
+                    cols = slice(PASS * a + P * t, PASS * a + P * (t + 1))
+                    nc.tensor.matmul_mx(
+                        out=a_bank[:, JB * t : JB * (t + 1)],
+                        lhsT=w1_codes[:, cols].bitcast(FP4X4), lhsT_scale=w1_planes[:, cols],
+                        rhs=v_w[a, h][:, js].bitcast(FP8X4), rhs_scale=v_sc[a, h][:, js],
+                        start=(a == 0), stop=(a == 1),
+                    )
+            w2_codes, w2_plane = w2_q[b]
+            for t in range(PACK):
+                cols = slice(P * t, P * (t + 1))
+                nc.tensor.matmul_mx(
+                    out=l_bank[:, JB * t : JB * (t + 1)],
+                    lhsT=w2_codes[:, cols].bitcast(FP8X4), lhsT_scale=w2_plane[:, cols],
+                    rhs=v2_w[h][:, js].bitcast(FP4X4), rhs_scale=v2_sc[h][:, js],
+                    start=True, stop=True,
+                )
+
+            def woven(ap):
+                return ap.rearrange("p (j t) -> p j t", t=PACK)
+
+            def factor(tile):
+                return tile[:, PACK * b : PACK * (b + 1)].unsqueeze(1).to_broadcast([P, JB, PACK])
+
+            load = l_bank[:].rearrange("p (t j) -> p j t", t=PACK)
+            gated = work.tile([P, PASS], F32, name="gated")
+            diff = work.tile([P, PASS], F32, name="diff")
+            sine = work.tile([P, PASS], F32, name="sine")
+            xz = work.tile([P, 2 * PASS], BF16, name="xz", align_bytes=64)
+            nc.scalar.activation(out=woven(gated[:]), in_=a_bank[:].rearrange("p (t j) -> p j t", t=PACK), func=ACT.Silu)
+            nc.vector.tensor_tensor(woven(xz[:, 0:PASS]), load, factor(gl_sb), ALU.mult)
+            nc.vector.tensor_tensor(woven(diff[:]), woven(gated[:]), load, ALU.subtract)
+            nc.scalar.activation(out=sine[:], in_=diff[:], func=ACT.Sin)
+            return sine, xz, woven, factor
+
+        def finish_first_stage(b, jb, state):
+            sine, xz, woven, factor = state
+            nc.vector.tensor_tensor(woven(xz[:, PASS : 2 * PASS]), woven(sine[:]), factor(gs_sb), ALU.mult)
+            xz_q[b, jb] = quantise("xz_%d_%d" % (b, jb), xz, 2 * JB)
+
+        y_banks = [psum2.tile([P, PASS], F32, name="y_bank%d" % jb) for jb in range(S // JB)]
+        y_scales = held("y_scales", S, U8)
+
+        def second_stage(b, jb):
+            codes, scales = xz_q[b, jb]
+            for t in range(PACK):
+                cols = slice(P * t, P * (t + 1))
+                nc.tensor.matmul_mx(
+                    out=y_banks[jb][:, JB * t : JB * (t + 1)],
+                    lhsT=w3_d[:, N * b + P * t : N * b + P * (t + 1)].bitcast(FP8X4),
+                    lhsT_scale=w3_sc_d[4 * b : P, cols],
+                    rhs=codes[:, 0:JB].bitcast(FP8X4), rhs_scale=scales[:, 0:JB],
+                    start=(b == 0 and t == 0), stop=False,
+                )
+            w4_codes, w4_plane = w4_q[b]
+            for t in range(PACK):
+                cols = slice(P * t, P * (t + 1))
+                nc.tensor.matmul_mx(
+                    out=y_banks[jb][:, JB * t : JB * (t + 1)],
+                    lhsT=w4_codes[:, cols].bitcast(FP8X4), lhsT_scale=w4_plane[:, cols],
+                    rhs=codes[:, JB : 2 * JB].bitcast(FP8X4), rhs_scale=scales[:, JB : 2 * JB],
+                    start=False, stop=(b == 1 and t == PACK - 1),
+                )
+
+        def hand_out(jb):
+            js = slice(JB * jb, JB * (jb + 1))
+            y = held("y%d" % jb, PACK * JB, F32)
+            nc.scalar.copy(out=y[:], in_=y_banks[jb][:])
+            nc.sync.dma_start(
+                out=out_0.rearrange("(p t) j -> p t j", t=PACK)[:, :, js],
+                in_=y[:].rearrange("p (t j) -> p t j", t=PACK),
+            )
+            y_bf = held("y_bf%d" % jb, PACK * JB, BF16)
+            if jb < S // JB - 1:
+                nc.scalar.copy(
+                    out=y_bf[:].rearrange("p (j t) -> p j t", t=PACK),
+                    in_=y_banks[jb][:].rearrange("p (t j) -> p j t", t=PACK),
+                )
+            else:
+                nc.vector.tensor_copy(
+                    out=y_bf[:].rearrange("p (c i t) -> p c t i", i=4, t=PACK),
+                    in_=y[:].rearrange("p (t c i) -> p c t i", i=4, t=PACK),
+                )
+            y_codes = held("y_codes%d" % jb, JB, U32)
+            nc.vector.quantize_mx(out=y_codes[:].bitcast(FP8X4), scales=y_scales[:, js], in_=y_bf[:])
+            nc.sync.dma_start(
+                out=out_1[0].rearrange("p m t -> p (m t)").bitcast(I32)[:, js], in_=y_codes[:].bitcast(I32))
+
+        chunks = [(b, jb) for b in range(2) for jb in range(S // JB)]
+        state = {}
+        w4_q = []
+        for step in range(len(chunks) + 1):
+            if step < len(chunks):
+                state[step] = first_stage(*chunks[step])
+            if step == 0:
+                w2_bf.append(round_and_deal("w2_1", w2_raw[1]))
+            if step == 2:
+                w2_q.append(quantise("w2_1", w2_bf[1], PASS))
+                w4_bf0 = round_and_deal("w4_0", w4_raw[0])
+            if step == 3:
+                w3_sc_d = deal("w3_sc_dealt", U8, w3_sc[:].rearrange("p (a n) -> p a n", a=1), 16)
+                w3_d = deal("w3_w_dealt", U32, w3_w[:].rearrange("p (a n) -> p a n", a=2), 4)
+            if step == 4:
+                w4_q.append(quantise("w4_0", w4_bf0, N))
+                w4_bf1 = round_and_deal("w4_1", w4_raw[1])
+            if step >= 1:
+                finish_first_stage(*chunks[step - 1], state[step - 1])
+            if step == 4:
+                for jb in range(S // JB):
+                    second_stage(0, jb)
+            if step == 5:
+                w4_q.append(quantise("w4_1", w4_bf1, N))
+            if step >= 5:
+                second_stage(1, step - 5)
+                hand_out(step - 5)
+
+        for q in range(QUADS):
+            nc.scalar.dma_start(
+                out=out_2[0, 4 * q : 4 * q + 4, :].bitcast(I32), in_=y_scales[32 * q : 32 * q + 4, :].bitcast(I32))

@@ -22,6 +22,7 @@ PASS = P * PACK
 QUADS = 4
 JB = 128
 HALF = 256
+PIECES = 2
 
 
 def tile_list_forklift_tipping_features_kernel(
@@ -53,16 +54,17 @@ def tile_list_forklift_tipping_features_kernel(
         gl_sb = held("gl_sb", 2 * PACK, F32)
         gs_sb = held("gs_sb", 2 * PACK, F32)
 
-        nc.vector.memset(tab2_sc[:].bitcast(I32), 0)
-        nc.vector.memset(tab_sc[:].bitcast(I32), 0)
         warm = held("warm", 16, F32)
         nc.gpsimd.memset(warm[:, 0:1], 0.0)
-        nc.gpsimd.memset(w1_sc[:].bitcast(I32), 0)
         nc.scalar.activation(out=warm[:, 8:9], in_=warm[:, 0:1], func=ACT.Silu)
+        nc.gpsimd.memset(tab_sc[:].bitcast(I32), 0)
+        nc.gpsimd.memset(w1_sc[:].bitcast(I32), 0)
+        nc.gpsimd.memset(tab2_sc[:].bitcast(I32), 0)
+        nc.gpsimd.memset(w3_sc[:].bitcast(I32), 0)
 
-        def load_scale_rows(queue, dst, src):
+        def load_scale_rows(dst, src):
             for q in range(QUADS):
-                queue.dma_start(
+                nc.sync.dma_start(
                     out=dst[32 * q : 32 * q + 4, :].bitcast(I32).rearrange("r (a n) -> r a n", a=src.shape[0]),
                     in_=src[:, 4 * q : 4 * q + 4, :].bitcast(I32).rearrange("a r n -> r a n"),
                 )
@@ -83,34 +85,41 @@ def tile_list_forklift_tipping_features_kernel(
             nc.sync.dma_start(
                 out=tab_w[a][:].bitcast(I32), in_=tab_words[a].rearrange("p n i -> p (n i)").bitcast(I32))
 
-        load_scale_rows(nc.gpsimd, w1_sc, w1_scales)
-        nc.gpsimd.memset(w3_sc[:].bitcast(I32), 0)
-        for q in range(QUADS):
-            nc.gpsimd.dma_start(
-                out=w3_sc[32 * q : 32 * q + 8, :].bitcast(I32),
-                in_=w3_scales[:, 4 * q : 4 * q + 4, :].bitcast(I32),
+        def load_factor(dst, src):
+            nc.sync.dma_start(
+                out=dst[:].rearrange("p (b t) -> p b t", b=2), in_=src.rearrange("(b p t) -> p b t", b=2, t=PACK))
+
+        def load_w3_scales():
+            for q in range(QUADS):
+                nc.sync.dma_start(
+                    out=w3_sc[32 * q : 32 * q + 8, :].bitcast(I32),
+                    in_=w3_scales[:, 4 * q : 4 * q + 4, :].bitcast(I32),
+                )
+
+        def load_w3_words():
+            nc.sync.dma_start(
+                out=w3_w[:].bitcast(I32).rearrange("p (a n) -> p a n", a=2),
+                in_=w3_words.rearrange("a p n i -> a p (n i)").bitcast(I32).rearrange("a p n -> p a n"),
             )
-        nc.sync.dma_start(out=tab2_w[:].bitcast(I32), in_=tab2_words[0].bitcast(I32))
+
         nc.sync.dma_start(idx2[:], offs2)
+        nc.sync.dma_start(out=tab2_w[:].bitcast(I32), in_=tab2_words[0].bitcast(I32))
         nc.sync.dma_start(idx[:], offs)
         load_tab_words(0)
-        load_scale_rows(nc.sync, tab2_sc, tab2_scales)
-        load_rows(w2_raw[0], w2[:, 0:PASS])
-        load_scale_rows(nc.sync, tab_sc, tab_scales)
+        load_scale_rows(tab2_sc, tab2_scales)
+        load_scale_rows(tab_sc, tab_scales)
         load_tab_words(1)
+        load_rows(w2_raw[0], w2[:, 0:PASS])
+        load_scale_rows(w1_sc, w1_scales)
         load_w1_words(0)
         load_w1_words(1)
-        nc.sync.dma_start(
-            out=gl_sb[:].rearrange("p (b t) -> p b t", b=2), in_=gl.rearrange("(b p t) -> p b t", b=2, t=PACK))
-        nc.sync.dma_start(
-            out=gs_sb[:].rearrange("p (b t) -> p b t", b=2), in_=gs.rearrange("(b p t) -> p b t", b=2, t=PACK))
+        load_factor(gl_sb, gl)
+        load_factor(gs_sb, gs)
         load_rows(w2_raw[1], w2[:, PASS : 2 * PASS])
-        nc.sync.dma_start(
-            out=w3_w[:].bitcast(I32).rearrange("p (a n) -> p a n", a=2),
-            in_=w3_words.rearrange("a p n i -> a p (n i)").bitcast(I32).rearrange("a p n -> p a n"),
-        )
-        for b in range(2):
-            load_rows(w4_raw[b], w4[PASS * b : PASS * (b + 1), :])
+        load_w3_scales()
+        load_w3_words()
+        load_rows(w4_raw[0], w4[0:PASS, :])
+        load_rows(w4_raw[1], w4[PASS : 2 * PASS, :])
 
         def gather(name, dtype, window, offsets, h):
             picked = held("%s_%d" % (name, h), HALF, dtype)
@@ -118,13 +127,12 @@ def tile_list_forklift_tipping_features_kernel(
             nc.vector.tensor_copy(picked[:], window.indirect(offsets[:, cols * h : cols * (h + 1)]))
             return picked
 
-        def round_and_deal(name, raw):
-            dealt = held(name + "_bf", PACK * PASS, BF16)
-            nc.scalar.copy(
-                out=dealt[:].rearrange("p (t m i) -> p m t i", t=PACK, i=PACK),
-                in_=raw[:].rearrange("p (i m t) -> p m t i", i=PACK, t=PACK),
+        def round_and_deal(dealt, raw, piece, copy):
+            ms = slice(P // PIECES * piece, P // PIECES * (piece + 1))
+            copy(
+                out=dealt[:].rearrange("p (t m i) -> p m t i", t=PACK, i=PACK)[:, ms],
+                in_=raw[:].rearrange("p (i m t) -> p m t i", i=PACK, t=PACK)[:, ms],
             )
-            return dealt
 
         def quantise(name, values, cols):
             codes = held(name + "_codes", cols, U32)
@@ -142,7 +150,10 @@ def tile_list_forklift_tipping_features_kernel(
             return dealt
 
         v_sc, v_w, v2_sc, v2_w = {}, {}, {}, {}
-        w2_bf = [round_and_deal("w2_%d" % b, w2_raw[b]) for b in range(1)]
+        w2_bf = [held("w2_bf%d" % b, PACK * PASS, BF16) for b in range(2)]
+        w4_bf = [held("w4_bf%d" % b, PACK * N, BF16) for b in range(2)]
+        for piece in range(PIECES):
+            round_and_deal(w2_bf[0], w2_raw[0], piece, nc.scalar.copy)
         def deal_w1_scales(b):
             return deal("w1_sc_dealt%d" % b, U8,
                         w1_sc[:].rearrange("p (a n) -> p a n", a=2)[:, :, PASS * b : PASS * (b + 1)], 16)
@@ -156,31 +167,43 @@ def tile_list_forklift_tipping_features_kernel(
             v_w[0, h] = gather("v_w0", U32, tab_w[0][:], idx, h)
         for h in range(2):
             v2_sc[h] = gather("v2_sc", U8, tab2_sc[:], idx2, h)
-        w1_sc_d = [deal_w1_scales(b) for b in range(2)]
+        w1_sc_d = [deal_w1_scales(0)]
+        w1_w_d = [deal_w1_words(0)]
+        v_w[1, 0] = gather("v_w1", U32, tab_w[1][:], idx, 0)
+        w2_q = [quantise("w2_0", w2_bf[0], PASS)]
         for a in range(2):
             v_sc[a, 0] = gather("v_sc%d" % a, U8, tab_sc[:, T * a : T * (a + 1)], idx, 0)
-        v_w[1, 0] = gather("v_w1", U32, tab_w[1][:], idx, 0)
-        w1_w_d = [deal_w1_words(0)]
-        w2_q = [quantise("w2_0", w2_bf[0], PASS)]
         for a in range(2):
             v_sc[a, 1] = gather("v_sc%d" % a, U8, tab_sc[:, T * a : T * (a + 1)], idx, 1)
         v_w[1, 1] = gather("v_w1", U32, tab_w[1][:], idx, 1)
+        w1_sc_d.append(deal_w1_scales(1))
         w1_w_d.append(deal_w1_words(1))
 
-        xz_q = {}
+        chunks = [(b, jb) for b in range(2) for jb in range(S // JB)]
+        banks, gated, diff, sine, xz, xz_q = {}, {}, {}, {}, {}, {}
 
-        def first_stage(b, jb):
+        def woven(ap):
+            return ap.rearrange("p (j t) -> p j t", t=PACK)
+
+        def weave(bank):
+            return bank[:].rearrange("p (t j) -> p j t", t=PACK)
+
+        def factor(tile, c):
+            b = chunks[c][0]
+            return tile[:, PACK * b : PACK * (b + 1)].unsqueeze(1).to_broadcast([P, JB, PACK])
+
+        def multiply(c):
+            b, jb = chunks[c]
             h, j0 = divmod(jb * JB, HALF)
             js = slice(j0, j0 + JB)
-            l_bank = psum1.tile([P, PASS], F32, name="l_bank")
             a_bank = psum1.tile([P, PASS], F32, name="a_bank")
-            w1_codes, w1_planes = w1_w_d[b], w1_sc_d[b]
+            l_bank = psum1.tile([P, PASS], F32, name="l_bank")
             for t in range(PACK):
                 for a in range(2):
                     cols = slice(PASS * a + P * t, PASS * a + P * (t + 1))
                     nc.tensor.matmul_mx(
                         out=a_bank[:, JB * t : JB * (t + 1)],
-                        lhsT=w1_codes[:, cols].bitcast(FP4X4), lhsT_scale=w1_planes[:, cols],
+                        lhsT=w1_w_d[b][:, cols].bitcast(FP4X4), lhsT_scale=w1_sc_d[b][:, cols],
                         rhs=v_w[a, h][:, js].bitcast(FP8X4), rhs_scale=v_sc[a, h][:, js],
                         start=(a == 0), stop=(a == 1),
                     )
@@ -193,31 +216,33 @@ def tile_list_forklift_tipping_features_kernel(
                     rhs=v2_w[h][:, js].bitcast(FP4X4), rhs_scale=v2_sc[h][:, js],
                     start=True, stop=True,
                 )
+            banks[c] = a_bank, l_bank
 
-            def woven(ap):
-                return ap.rearrange("p (j t) -> p j t", t=PACK)
+        def gate(c):
+            gated[c] = work.tile([P, PASS], F32, name="gated")
+            nc.scalar.activation(out=woven(gated[c][:]), in_=weave(banks[c][0]), func=ACT.Silu)
 
-            def factor(tile):
-                return tile[:, PACK * b : PACK * (b + 1)].unsqueeze(1).to_broadcast([P, JB, PACK])
+        def subtract(c):
+            diff[c] = work.tile([P, PASS], F32, name="diff")
+            nc.vector.tensor_tensor(woven(diff[c][:]), woven(gated[c][:]), weave(banks[c][1]), ALU.subtract)
 
-            load = l_bank[:].rearrange("p (t j) -> p j t", t=PACK)
-            gated = work.tile([P, PASS], F32, name="gated")
-            diff = work.tile([P, PASS], F32, name="diff")
-            sine = work.tile([P, PASS], F32, name="sine")
-            xz = work.tile([P, 2 * PASS], BF16, name="xz", align_bytes=64)
-            nc.scalar.activation(out=woven(gated[:]), in_=a_bank[:].rearrange("p (t j) -> p j t", t=PACK), func=ACT.Silu)
-            nc.vector.tensor_tensor(woven(xz[:, 0:PASS]), load, factor(gl_sb), ALU.mult)
-            nc.vector.tensor_tensor(woven(diff[:]), woven(gated[:]), load, ALU.subtract)
-            nc.scalar.activation(out=sine[:], in_=diff[:], func=ACT.Sin)
-            return sine, xz, woven, factor
+        def scale_load(c):
+            xz[c] = work.tile([P, 2 * PASS], BF16, name="xz", align_bytes=64, bufs=4)
+            nc.vector.tensor_tensor(woven(xz[c][:, 0:PASS]), weave(banks[c][1]), factor(gl_sb, c), ALU.mult)
 
-        def finish_first_stage(b, jb, state):
-            sine, xz, woven, factor = state
-            nc.vector.tensor_tensor(woven(xz[:, PASS : 2 * PASS]), woven(sine[:]), factor(gs_sb), ALU.mult)
-            xz_q[b, jb] = quantise("xz_%d_%d" % (b, jb), xz, 2 * JB)
+        def take_sine(c):
+            sine[c] = work.tile([P, PASS], F32, name="sine")
+            nc.scalar.activation(out=sine[c][:], in_=diff[c][:], func=ACT.Sin)
+
+        def scale_sine(c):
+            nc.vector.tensor_tensor(woven(xz[c][:, PASS : 2 * PASS]), woven(sine[c][:]), factor(gs_sb, c), ALU.mult)
+
+        def quantise_chunk(c):
+            xz_q[chunks[c]] = quantise("xz_%d" % c, xz[c], 2 * JB)
 
         y_banks = [psum2.tile([P, PASS], F32, name="y_bank%d" % jb) for jb in range(S // JB)]
         y_scales = held("y_scales", S, U8)
+        y_codes = held("y_codes", S, U32)
 
         def second_stage(b, jb):
             codes, scales = xz_q[b, jb]
@@ -249,7 +274,7 @@ def tile_list_forklift_tipping_features_kernel(
                 in_=y[:].rearrange("p (t j) -> p t j", t=PACK),
             )
             y_bf = held("y_bf%d" % jb, PACK * JB, BF16)
-            if jb < S // JB - 1:
+            if jb < 2:
                 nc.scalar.copy(
                     out=y_bf[:].rearrange("p (j t) -> p j t", t=PACK),
                     in_=y_banks[jb][:].rearrange("p (t j) -> p j t", t=PACK),
@@ -259,38 +284,46 @@ def tile_list_forklift_tipping_features_kernel(
                     out=y_bf[:].rearrange("p (c i t) -> p c t i", i=4, t=PACK),
                     in_=y[:].rearrange("p (t c i) -> p c t i", i=4, t=PACK),
                 )
-            y_codes = held("y_codes%d" % jb, JB, U32)
-            nc.vector.quantize_mx(out=y_codes[:].bitcast(FP8X4), scales=y_scales[:, js], in_=y_bf[:])
-            nc.sync.dma_start(
-                out=out_1[0].rearrange("p m t -> p (m t)").bitcast(I32)[:, js], in_=y_codes[:].bitcast(I32))
+            nc.vector.quantize_mx(out=y_codes[:, js].bitcast(FP8X4), scales=y_scales[:, js], in_=y_bf[:])
+            if jb % 2 == 1:
+                pair = slice(JB * (jb - 1), JB * (jb + 1))
+                nc.sync.dma_start(
+                    out=out_1[0].rearrange("p m t -> p (m t)").bitcast(I32)[:, pair], in_=y_codes[:, pair].bitcast(I32))
 
-        chunks = [(b, jb) for b in range(2) for jb in range(S // JB)]
-        state = {}
         w4_q = []
-        for step in range(len(chunks) + 1):
-            if step < len(chunks):
-                state[step] = first_stage(*chunks[step])
-            if step == 0:
-                w2_bf.append(round_and_deal("w2_1", w2_raw[1]))
+        count = len(chunks)
+        rounding = [(w2_bf[1], w2_raw[1])] + [(w4_bf[b], w4_raw[b]) for b in range(2)]
+        pieces = [(dealt, raw, piece) for dealt, raw in rounding for piece in range(PIECES)]
+        for step in range(count + 2):
+            if step < count:
+                multiply(step)
+            if 0 <= step - 1 < count:
+                subtract(step - 1)
+            if step < count:
+                gate(step)
+            if 0 <= step - 1 < count:
+                scale_load(step - 1)
+                take_sine(step - 1)
+            if 0 <= step - 2 < count:
+                scale_sine(step - 2)
+            for dealt, raw, piece in pieces[step : step + 1]:
+                round_and_deal(dealt, raw, piece, nc.scalar.copy)
             if step == 2:
                 w2_q.append(quantise("w2_1", w2_bf[1], PASS))
-                w4_bf0 = round_and_deal("w4_0", w4_raw[0])
             if step == 3:
                 w3_sc_d = deal("w3_sc_dealt", U8, w3_sc[:].rearrange("p (a n) -> p a n", a=1), 16)
                 w3_d = deal("w3_w_dealt", U32, w3_w[:].rearrange("p (a n) -> p a n", a=2), 4)
             if step == 4:
-                w4_q.append(quantise("w4_0", w4_bf0, N))
-                w4_bf1 = round_and_deal("w4_1", w4_raw[1])
-            if step >= 1:
-                finish_first_stage(*chunks[step - 1], state[step - 1])
-            if step == 4:
-                for jb in range(S // JB):
-                    second_stage(0, jb)
-            if step == 5:
-                w4_q.append(quantise("w4_1", w4_bf1, N))
-            if step >= 5:
-                second_stage(1, step - 5)
-                hand_out(step - 5)
+                w4_q.append(quantise("w4_0", w4_bf[0], N))
+            if step == 6:
+                w4_q.append(quantise("w4_1", w4_bf[1], N))
+            if 0 <= step - 2 < count:
+                quantise_chunk(step - 2)
+            if 4 <= step < 8:
+                second_stage(0, step - 4)
+            if step >= 4 + 2:
+                second_stage(1, step - 4 - 2)
+                hand_out(step - 4 - 2)
 
         for q in range(QUADS):
             nc.scalar.dma_start(

@@ -19,10 +19,14 @@ ALU = mybir.AluOpType
 P = 128
 PACK = 4
 PASS = P * PACK
-QUADS = 4
-JB = 128
-HALF = 256
+QUADRANTS = 4
+ROWS = 4
+TRIPS = 128
+BLOCKS = S // TRIPS
+GROUPS = H // PASS
+LINE = 16
 PIECES = 2
+SCALAR_BLOCKS = 2
 
 
 def tile_list_forklift_tipping_features_kernel(
@@ -33,298 +37,264 @@ def tile_list_forklift_tipping_features_kernel(
     with ExitStack() as ctx:
         keep = ctx.enter_context(tc.tile_pool(name="keep", bufs=1))
         work = ctx.enter_context(tc.tile_pool(name="work", bufs=3))
-        psum1 = ctx.enter_context(tc.psum_pool(name="psum1", bufs=2))
-        psum2 = ctx.enter_context(tc.psum_pool(name="psum2", bufs=1))
+        first_psum = ctx.enter_context(tc.psum_pool(name="first_psum", bufs=2))
+        second_psum = ctx.enter_context(tc.psum_pool(name="second_psum", bufs=1))
 
-        def held(name, cols, dtype):
-            return keep.tile([P, cols], dtype, name=name, align_bytes=64)
+        def held(name, columns, dtype):
+            return keep.tile([P, columns], dtype, name=name, align_bytes=64)
 
         idx = keep.tile([P, S // 16], U16, name="idx")
         idx2 = keep.tile([P, S // 16], U16, name="idx2")
+        tab_w = [held("tab_w%d" % k, T, U32) for k in range(2)]
         tab_sc = held("tab_sc", 2 * T, U8)
-        tab2_sc = held("tab2_sc", T2, U8)
-        w1_sc = held("w1_sc", 2 * H, U8)
-        w3_sc = held("w3_sc", N, U8)
-        tab_w = [held("tab_w%d" % a, T, U32) for a in range(2)]
         tab2_w = held("tab2_w", T2, U16)
-        w1_w = [held("w1_w%d" % b, 2 * PASS, U16) for b in range(2)]
-        w3_w = held("w3_w", 2 * N, U32)
-        w2_raw = [held("w2_raw%d" % b, PACK * PASS, F32) for b in range(2)]
-        w4_raw = [held("w4_raw%d" % b, PACK * N, F32) for b in range(2)]
-        gl_sb = held("gl_sb", 2 * PACK, F32)
-        gs_sb = held("gs_sb", 2 * PACK, F32)
+        tab2_sc = held("tab2_sc", T2, U8)
+        w1_w = held("w1_w", 2 * H, U16)
+        w1_sc = held("w1_sc", 2 * H, U8)
+        w3_w = held("w3_w", GROUPS * N, U32)
+        w3_sc = held("w3_sc", N, U8)
+        w2_raw = [held("w2_raw%d" % g, PACK * PASS, F32) for g in range(GROUPS)]
+        w4_raw = [held("w4_raw%d" % g, PACK * N, F32) for g in range(GROUPS)]
+        gl_sb = held("gl_sb", GROUPS * PACK, F32)
+        gs_sb = held("gs_sb", GROUPS * PACK, F32)
 
         warm = held("warm", 16, F32)
         nc.gpsimd.memset(warm[:, 0:1], 0.0)
         nc.scalar.activation(out=warm[:, 8:9], in_=warm[:, 0:1], func=ACT.Silu)
+
         nc.gpsimd.memset(tab_sc[:].bitcast(I32), 0)
+        nc.vector.memset(tab2_sc[:].bitcast(I32), 0)
         nc.gpsimd.memset(w1_sc[:].bitcast(I32), 0)
-        nc.gpsimd.memset(tab2_sc[:].bitcast(I32), 0)
         nc.gpsimd.memset(w3_sc[:].bitcast(I32), 0)
 
-        def load_scale_rows(dst, src):
-            for q in range(QUADS):
+        def load_words(tile, words):
+            nc.sync.dma_start(
+                out=tile[:].bitcast(I32).rearrange("p (g c) -> p g c", g=words.shape[0]),
+                in_=words.bitcast(I32).rearrange("g p c -> p g c"),
+            )
+
+        def load_planes(tile, scales):
+            for q in range(QUADRANTS):
                 nc.sync.dma_start(
-                    out=dst[32 * q : 32 * q + 4, :].bitcast(I32).rearrange("r (a n) -> r a n", a=src.shape[0]),
-                    in_=src[:, 4 * q : 4 * q + 4, :].bitcast(I32).rearrange("a r n -> r a n"),
+                    out=tile[32 * q : 32 * q + ROWS, :].bitcast(I32).rearrange("r (g c) -> r g c", g=scales.shape[0]),
+                    in_=scales[:, ROWS * q : ROWS * (q + 1), :].bitcast(I32).rearrange("g r c -> r g c"),
                 )
 
-        def load_rows(dst, src):
-            nc.sync.dma_start(
-                out=dst[:].rearrange("p (i c) -> p i c", i=PACK),
-                in_=src.rearrange("(p i) c -> p i c", i=PACK),
-            )
-
-        def load_w1_words(b):
-            nc.sync.dma_start(
-                out=w1_w[b][:].bitcast(I32).rearrange("p (a n) -> p a n", a=2),
-                in_=w1_words[:, :, 2 * PASS * b : 2 * PASS * (b + 1)].bitcast(I32).rearrange("a p n -> p a n"),
-            )
-
-        def load_tab_words(a):
-            nc.sync.dma_start(
-                out=tab_w[a][:].bitcast(I32), in_=tab_words[a].rearrange("p n i -> p (n i)").bitcast(I32))
-
-        def load_factor(dst, src):
-            nc.sync.dma_start(
-                out=dst[:].rearrange("p (b t) -> p b t", b=2), in_=src.rearrange("(b p t) -> p b t", b=2, t=PACK))
-
-        def load_w3_scales():
-            for q in range(QUADS):
+        def load_stacked_planes(tile, scales):
+            for q in range(QUADRANTS):
                 nc.sync.dma_start(
-                    out=w3_sc[32 * q : 32 * q + 8, :].bitcast(I32),
-                    in_=w3_scales[:, 4 * q : 4 * q + 4, :].bitcast(I32),
+                    out=tile[32 * q : 32 * q + GROUPS * ROWS, :].bitcast(I32),
+                    in_=scales[:, ROWS * q : ROWS * (q + 1), :].bitcast(I32),
                 )
 
-        def load_w3_words():
+        def load_rows(tile, rows):
             nc.sync.dma_start(
-                out=w3_w[:].bitcast(I32).rearrange("p (a n) -> p a n", a=2),
-                in_=w3_words.rearrange("a p n i -> a p (n i)").bitcast(I32).rearrange("a p n -> p a n"),
-            )
+                out=tile[:].rearrange("p (i c) -> p i c", i=PACK), in_=rows.rearrange("(p i) c -> p i c", i=PACK))
 
-        nc.sync.dma_start(idx2[:], offs2)
-        nc.sync.dma_start(out=tab2_w[:].bitcast(I32), in_=tab2_words[0].bitcast(I32))
+        def load_factor(tile, factor):
+            nc.sync.dma_start(
+                out=tile[:].rearrange("p (g t) -> p g t", t=PACK), in_=factor.rearrange("(g p t) -> p g t", p=P, t=PACK))
+
         nc.sync.dma_start(idx[:], offs)
-        load_tab_words(0)
-        load_scale_rows(tab2_sc, tab2_scales)
-        load_scale_rows(tab_sc, tab_scales)
-        load_tab_words(1)
+        nc.sync.dma_start(idx2[:], offs2)
+        load_words(tab_w[0], tab_words[0:1].rearrange("g p c i -> g p (c i)"))
+        load_planes(tab_sc, tab_scales)
+        load_planes(tab2_sc, tab2_scales)
+        load_planes(w1_sc, w1_scales)
+        load_words(tab_w[1], tab_words[1:2].rearrange("g p c i -> g p (c i)"))
         load_rows(w2_raw[0], w2[:, 0:PASS])
-        load_scale_rows(w1_sc, w1_scales)
-        load_w1_words(0)
-        load_w1_words(1)
+        load_words(w1_w, w1_words)
+        load_words(tab2_w, tab2_words)
         load_factor(gl_sb, gl)
         load_factor(gs_sb, gs)
         load_rows(w2_raw[1], w2[:, PASS : 2 * PASS])
-        load_w3_scales()
-        load_w3_words()
+        load_stacked_planes(w3_sc, w3_scales)
+        load_words(w3_w, w3_words.rearrange("g p c i -> g p (c i)"))
         load_rows(w4_raw[0], w4[0:PASS, :])
         load_rows(w4_raw[1], w4[PASS : 2 * PASS, :])
 
-        def gather(name, dtype, window, offsets, h):
-            picked = held("%s_%d" % (name, h), HALF, dtype)
-            cols = HALF // 16
-            nc.vector.tensor_copy(picked[:], window.indirect(offsets[:, cols * h : cols * (h + 1)]))
+        def gather(name, dtype, window, offsets):
+            picked = held(name, S, dtype)
+            nc.vector.tensor_copy(picked[:], window.indirect(offsets[:]))
             return picked
 
-        def round_and_deal(dealt, raw, piece, copy):
-            ms = slice(P // PIECES * piece, P // PIECES * (piece + 1))
-            copy(
-                out=dealt[:].rearrange("p (t m i) -> p m t i", t=PACK, i=PACK)[:, ms],
-                in_=raw[:].rearrange("p (i m t) -> p m t i", i=PACK, t=PACK)[:, ms],
-            )
-
-        def quantise(name, values, cols):
-            codes = held(name + "_codes", cols, U32)
-            scales = held(name + "_scales", cols, U8)
-            nc.vector.quantize_mx(out=codes[:].bitcast(FP8X4), scales=scales[:], in_=values[:])
-            return codes, scales
-
-        def deal(name, dtype, src, run):
-            passes = src.shape[1]
-            dealt = held(name, passes * PASS, dtype)
+        def deal(name, dtype, size, packed):
+            run = LINE // size
+            groups = packed.shape[1]
+            dealt = held(name, groups * PASS, dtype)
             nc.vector.tensor_copy(
-                out=dealt[:].rearrange("p (a t c i) -> p a c t i", a=passes, t=PACK, i=run),
-                in_=src.rearrange("p a (c i t) -> p a c t i", t=PACK, i=run),
+                out=dealt[:].rearrange("p (g t c u) -> p g c t u", g=groups, t=PACK, u=run),
+                in_=packed.rearrange("p g (c u t) -> p g c t u", t=PACK, u=run),
             )
             return dealt
 
-        v_sc, v_w, v2_sc, v2_w = {}, {}, {}, {}
-        w2_bf = [held("w2_bf%d" % b, PACK * PASS, BF16) for b in range(2)]
-        w4_bf = [held("w4_bf%d" % b, PACK * N, BF16) for b in range(2)]
-        for piece in range(PIECES):
-            round_and_deal(w2_bf[0], w2_raw[0], piece, nc.scalar.copy)
-        def deal_w1_scales(b):
-            return deal("w1_sc_dealt%d" % b, U8,
-                        w1_sc[:].rearrange("p (a n) -> p a n", a=2)[:, :, PASS * b : PASS * (b + 1)], 16)
+        def by_group(tile):
+            return tile[:].rearrange("p (g c) -> p g c", c=PASS)
 
-        def deal_w1_words(b):
-            return deal("w1_w_dealt%d" % b, U16, w1_w[b][:].rearrange("p (a n) -> p a n", a=2), 8)
+        def round_and_deal(rounded, raw, part):
+            nc.scalar.copy(
+                out=rounded[:].rearrange("p (s e m i) -> p s m i e", s=2, e=2, i=PACK)[:, :, part],
+                in_=raw[:].rearrange("p (i m s e) -> p s m i e", i=PACK, s=2, e=2)[:, :, part],
+            )
 
-        for h in range(2):
-            v2_w[h] = gather("v2_w", U16, tab2_w[:], idx2, h)
-        for h in range(2):
-            v_w[0, h] = gather("v_w0", U32, tab_w[0][:], idx, h)
-        for h in range(2):
-            v2_sc[h] = gather("v2_sc", U8, tab2_sc[:], idx2, h)
-        w1_sc_d = [deal_w1_scales(0)]
-        w1_w_d = [deal_w1_words(0)]
-        v_w[1, 0] = gather("v_w1", U32, tab_w[1][:], idx, 0)
+        def quantise(name, values, columns):
+            codes = held(name + "_codes", columns, U32)
+            plane = held(name + "_plane", columns, U8)
+            nc.vector.quantize_mx(out=codes[:].bitcast(FP8X4), scales=plane[:], in_=values[:])
+            return codes, plane
+
+        w2_bf = [held("w2_bf%d" % g, PACK * PASS, BF16) for g in range(GROUPS)]
+        w4_bf = [held("w4_bf%d" % g, PACK * N, BF16) for g in range(GROUPS)]
+        round_and_deal(w2_bf[0], w2_raw[0], slice(0, P))
+        v_w = [gather("v_w0", U32, tab_w[0][:], idx)]
+        v_sc = [gather("v_sc%d" % k, U8, tab_sc[:, T * k : T * (k + 1)], idx) for k in range(2)]
+        v2_sc = gather("v2_sc", U8, tab2_sc[:], idx2)
+        w1_sc_dealt = deal("w1_sc_dealt", U8, 1, by_group(w1_sc))
+        v_w.append(gather("v_w1", U32, tab_w[1][:], idx))
+        w1_w_dealt = [deal("w1_w_dealt0", U16, 2, by_group(w1_w)[:, 0::GROUPS])]
+        v2_w = gather("v2_w", U16, tab2_w[:], idx2)
         w2_q = [quantise("w2_0", w2_bf[0], PASS)]
-        for a in range(2):
-            v_sc[a, 0] = gather("v_sc%d" % a, U8, tab_sc[:, T * a : T * (a + 1)], idx, 0)
-        for a in range(2):
-            v_sc[a, 1] = gather("v_sc%d" % a, U8, tab_sc[:, T * a : T * (a + 1)], idx, 1)
-        v_w[1, 1] = gather("v_w1", U32, tab_w[1][:], idx, 1)
-        w1_sc_d.append(deal_w1_scales(1))
-        w1_w_d.append(deal_w1_words(1))
+        w1_w_dealt.append(deal("w1_w_dealt1", U16, 2, by_group(w1_w)[:, 1::GROUPS]))
+        w4_q = []
 
-        chunks = [(b, jb) for b in range(2) for jb in range(S // JB)]
+        chunks = [(g, b) for g in range(GROUPS) for b in range(BLOCKS)]
         banks, gated, diff, sine, xz, xz_q = {}, {}, {}, {}, {}, {}
 
-        def woven(ap):
-            return ap.rearrange("p (j t) -> p j t", t=PACK)
+        def from_bank(bank):
+            return bank[:].rearrange("p (t c e) -> p c t e", t=PACK, e=2)
 
-        def weave(bank):
-            return bank[:].rearrange("p (t j) -> p j t", t=PACK)
+        def as_walked(tile):
+            return tile[:].rearrange("p (c t e) -> p c t e", t=PACK, e=2)
+
+        def to_words(columns):
+            return columns.rearrange("p (c e t) -> p c t e", t=PACK, e=2)
 
         def factor(tile, c):
-            b = chunks[c][0]
-            return tile[:, PACK * b : PACK * (b + 1)].unsqueeze(1).to_broadcast([P, JB, PACK])
+            g = chunks[c][0]
+            return tile[:, PACK * g : PACK * (g + 1)].unsqueeze(1).unsqueeze(3).to_broadcast([P, TRIPS // 2, PACK, 2])
 
-        def multiply(c):
-            b, jb = chunks[c]
-            h, j0 = divmod(jb * JB, HALF)
-            js = slice(j0, j0 + JB)
-            a_bank = psum1.tile([P, PASS], F32, name="a_bank")
-            l_bank = psum1.tile([P, PASS], F32, name="l_bank")
+        def multiply_first(c):
+            g, b = chunks[c]
+            trips = slice(TRIPS * b, TRIPS * (b + 1))
+            a_bank = first_psum.tile([P, PASS], F32, name="a_bank")
+            load_bank = first_psum.tile([P, PASS], F32, name="load_bank")
             for t in range(PACK):
-                for a in range(2):
-                    cols = slice(PASS * a + P * t, PASS * a + P * (t + 1))
+                for k in range(2):
+                    first = H * k + PASS * g + P * t
                     nc.tensor.matmul_mx(
-                        out=a_bank[:, JB * t : JB * (t + 1)],
-                        lhsT=w1_w_d[b][:, cols].bitcast(FP4X4), lhsT_scale=w1_sc_d[b][:, cols],
-                        rhs=v_w[a, h][:, js].bitcast(FP8X4), rhs_scale=v_sc[a, h][:, js],
-                        start=(a == 0), stop=(a == 1),
+                        out=a_bank[:, TRIPS * t : TRIPS * (t + 1)],
+                        lhsT=w1_w_dealt[g][:, PASS * k + P * t : PASS * k + P * (t + 1)].bitcast(FP4X4),
+                        lhsT_scale=w1_sc_dealt[:, first : first + P],
+                        rhs=v_w[k][:, trips].bitcast(FP8X4), rhs_scale=v_sc[k][:, trips],
+                        start=(k == 0), stop=(k == 1),
                     )
-            w2_codes, w2_plane = w2_q[b]
+            codes, plane = w2_q[g]
             for t in range(PACK):
-                cols = slice(P * t, P * (t + 1))
                 nc.tensor.matmul_mx(
-                    out=l_bank[:, JB * t : JB * (t + 1)],
-                    lhsT=w2_codes[:, cols].bitcast(FP8X4), lhsT_scale=w2_plane[:, cols],
-                    rhs=v2_w[h][:, js].bitcast(FP4X4), rhs_scale=v2_sc[h][:, js],
+                    out=load_bank[:, TRIPS * t : TRIPS * (t + 1)],
+                    lhsT=codes[:, P * t : P * (t + 1)].bitcast(FP8X4), lhsT_scale=plane[:, P * t : P * (t + 1)],
+                    rhs=v2_w[:, trips].bitcast(FP4X4), rhs_scale=v2_sc[:, trips],
                     start=True, stop=True,
                 )
-            banks[c] = a_bank, l_bank
+            banks[c] = a_bank, load_bank
 
         def gate(c):
             gated[c] = work.tile([P, PASS], F32, name="gated")
-            nc.scalar.activation(out=woven(gated[c][:]), in_=weave(banks[c][0]), func=ACT.Silu)
+            nc.scalar.activation(out=as_walked(gated[c]), in_=from_bank(banks[c][0]), func=ACT.Silu)
 
         def subtract(c):
             diff[c] = work.tile([P, PASS], F32, name="diff")
-            nc.vector.tensor_tensor(woven(diff[c][:]), woven(gated[c][:]), weave(banks[c][1]), ALU.subtract)
+            nc.vector.tensor_tensor(as_walked(diff[c]), as_walked(gated[c]), from_bank(banks[c][1]), ALU.subtract)
 
-        def scale_load(c):
+        def make_x(c):
             xz[c] = work.tile([P, 2 * PASS], BF16, name="xz", align_bytes=64, bufs=4)
-            nc.vector.tensor_tensor(woven(xz[c][:, 0:PASS]), weave(banks[c][1]), factor(gl_sb, c), ALU.mult)
+            nc.vector.tensor_tensor(to_words(xz[c][:, 0:PASS]), from_bank(banks[c][1]), factor(gl_sb, c), ALU.mult)
 
         def take_sine(c):
             sine[c] = work.tile([P, PASS], F32, name="sine")
             nc.scalar.activation(out=sine[c][:], in_=diff[c][:], func=ACT.Sin)
 
-        def scale_sine(c):
-            nc.vector.tensor_tensor(woven(xz[c][:, PASS : 2 * PASS]), woven(sine[c][:]), factor(gs_sb, c), ALU.mult)
+        def make_z(c):
+            nc.vector.tensor_tensor(to_words(xz[c][:, PASS : 2 * PASS]), as_walked(sine[c]), factor(gs_sb, c), ALU.mult)
 
         def quantise_chunk(c):
-            xz_q[chunks[c]] = quantise("xz_%d" % c, xz[c], 2 * JB)
+            xz_q[chunks[c]] = quantise("xz%d" % c, xz[c], 2 * TRIPS)
 
-        y_banks = [psum2.tile([P, PASS], F32, name="y_bank%d" % jb) for jb in range(S // JB)]
-        y_scales = held("y_scales", S, U8)
+        y_banks = [second_psum.tile([P, PASS], F32, name="y_bank%d" % b) for b in range(BLOCKS)]
         y_codes = held("y_codes", S, U32)
+        y_plane = held("y_plane", S, U8)
 
-        def second_stage(b, jb):
-            codes, scales = xz_q[b, jb]
+        def multiply_second(g, b):
+            codes, plane = xz_q[g, b]
             for t in range(PACK):
-                cols = slice(P * t, P * (t + 1))
                 nc.tensor.matmul_mx(
-                    out=y_banks[jb][:, JB * t : JB * (t + 1)],
-                    lhsT=w3_d[:, N * b + P * t : N * b + P * (t + 1)].bitcast(FP8X4),
-                    lhsT_scale=w3_sc_d[4 * b : P, cols],
-                    rhs=codes[:, 0:JB].bitcast(FP8X4), rhs_scale=scales[:, 0:JB],
-                    start=(b == 0 and t == 0), stop=False,
+                    out=y_banks[b][:, TRIPS * t : TRIPS * (t + 1)],
+                    lhsT=w3_w_dealt[:, N * g + P * t : N * g + P * (t + 1)].bitcast(FP8X4),
+                    lhsT_scale=w3_sc_dealt[ROWS * g : P, P * t : P * (t + 1)],
+                    rhs=codes[:, 0:TRIPS].bitcast(FP8X4), rhs_scale=plane[:, 0:TRIPS],
+                    start=(g == 0 and t == 0), stop=False,
                 )
-            w4_codes, w4_plane = w4_q[b]
+            w4_codes, w4_plane = w4_q[g]
             for t in range(PACK):
-                cols = slice(P * t, P * (t + 1))
                 nc.tensor.matmul_mx(
-                    out=y_banks[jb][:, JB * t : JB * (t + 1)],
-                    lhsT=w4_codes[:, cols].bitcast(FP8X4), lhsT_scale=w4_plane[:, cols],
-                    rhs=codes[:, JB : 2 * JB].bitcast(FP8X4), rhs_scale=scales[:, JB : 2 * JB],
-                    start=False, stop=(b == 1 and t == PACK - 1),
+                    out=y_banks[b][:, TRIPS * t : TRIPS * (t + 1)],
+                    lhsT=w4_codes[:, P * t : P * (t + 1)].bitcast(FP8X4), lhsT_scale=w4_plane[:, P * t : P * (t + 1)],
+                    rhs=codes[:, TRIPS : 2 * TRIPS].bitcast(FP8X4), rhs_scale=plane[:, TRIPS : 2 * TRIPS],
+                    start=False, stop=(g == GROUPS - 1 and t == PACK - 1),
                 )
 
-        def hand_out(jb):
-            js = slice(JB * jb, JB * (jb + 1))
-            y = held("y%d" % jb, PACK * JB, F32)
-            nc.scalar.copy(out=y[:], in_=y_banks[jb][:])
+        def hand_out(b):
+            trips = slice(TRIPS * b, TRIPS * (b + 1))
+            y = held("y%d" % b, PACK * TRIPS, F32)
+            nc.scalar.copy(out=y[:], in_=y_banks[b][:])
             nc.sync.dma_start(
-                out=out_0.rearrange("(p t) j -> p t j", t=PACK)[:, :, js],
+                out=out_0.rearrange("(p t) j -> p t j", t=PACK)[:, :, trips],
                 in_=y[:].rearrange("p (t j) -> p t j", t=PACK),
             )
-            y_bf = held("y_bf%d" % jb, PACK * JB, BF16)
-            if jb < 2:
-                nc.scalar.copy(
-                    out=y_bf[:].rearrange("p (j t) -> p j t", t=PACK),
-                    in_=y_banks[jb][:].rearrange("p (t j) -> p j t", t=PACK),
-                )
+            y_bf = held("y_bf%d" % b, PACK * TRIPS, BF16)
+            if b < SCALAR_BLOCKS:
+                nc.scalar.copy(out=to_words(y_bf[:]), in_=from_bank(y_banks[b]))
             else:
-                nc.vector.tensor_copy(
-                    out=y_bf[:].rearrange("p (c i t) -> p c t i", i=4, t=PACK),
-                    in_=y[:].rearrange("p (t c i) -> p c t i", i=4, t=PACK),
-                )
-            nc.vector.quantize_mx(out=y_codes[:, js].bitcast(FP8X4), scales=y_scales[:, js], in_=y_bf[:])
-            if jb % 2 == 1:
-                pair = slice(JB * (jb - 1), JB * (jb + 1))
+                nc.vector.tensor_copy(out=to_words(y_bf[:]), in_=from_bank(y))
+            nc.vector.quantize_mx(out=y_codes[:, trips].bitcast(FP8X4), scales=y_plane[:, trips], in_=y_bf[:])
+            if b % 2 == 1:
+                pair = slice(TRIPS * (b - 1), TRIPS * (b + 1))
                 nc.sync.dma_start(
                     out=out_1[0].rearrange("p m t -> p (m t)").bitcast(I32)[:, pair], in_=y_codes[:, pair].bitcast(I32))
 
-        w4_q = []
+        late = [("w2_1", w2_bf[1], w2_raw[1], w2_q), ("w4_0", w4_bf[0], w4_raw[0], w4_q), ("w4_1", w4_bf[1], w4_raw[1], w4_q)]
         count = len(chunks)
-        rounding = [(w2_bf[1], w2_raw[1])] + [(w4_bf[b], w4_raw[b]) for b in range(2)]
-        pieces = [(dealt, raw, piece) for dealt, raw in rounding for piece in range(PIECES)]
         for step in range(count + 2):
             if step < count:
-                multiply(step)
-            if 0 <= step - 1 < count:
+                multiply_first(step)
+            if 1 <= step <= count:
                 subtract(step - 1)
             if step < count:
                 gate(step)
-            if 0 <= step - 1 < count:
-                scale_load(step - 1)
+            if 1 <= step <= count:
+                make_x(step - 1)
                 take_sine(step - 1)
-            if 0 <= step - 2 < count:
-                scale_sine(step - 2)
-            for dealt, raw, piece in pieces[step : step + 1]:
-                round_and_deal(dealt, raw, piece, nc.scalar.copy)
-            if step == 2:
-                w2_q.append(quantise("w2_1", w2_bf[1], PASS))
-            if step == 3:
-                w3_sc_d = deal("w3_sc_dealt", U8, w3_sc[:].rearrange("p (a n) -> p a n", a=1), 16)
-                w3_d = deal("w3_w_dealt", U32, w3_w[:].rearrange("p (a n) -> p a n", a=2), 4)
-            if step == 4:
-                w4_q.append(quantise("w4_0", w4_bf[0], N))
-            if step == 6:
-                w4_q.append(quantise("w4_1", w4_bf[1], N))
-            if 0 <= step - 2 < count:
+            if step >= 2:
+                make_z(step - 2)
+            weight, piece = divmod(step, PIECES)
+            if weight < len(late):
+                round_and_deal(late[weight][1], late[weight][2], slice(P // PIECES * piece, P // PIECES * (piece + 1)))
+            if piece == 0 and 1 <= weight <= len(late):
+                name, rounded, raw, quantised = late[weight - 1]
+                quantised.append(quantise(name, rounded, PASS))
+            if step == BLOCKS - 1:
+                w3_sc_dealt = deal("w3_sc_dealt", U8, 1, by_group(w3_sc))
+                w3_w_dealt = deal("w3_w_dealt", U32, 4, by_group(w3_w))
+            if step >= 2:
                 quantise_chunk(step - 2)
-            if 4 <= step < 8:
-                second_stage(0, step - 4)
-            if step >= 4 + 2:
-                second_stage(1, step - 4 - 2)
-                hand_out(step - 4 - 2)
+            if BLOCKS <= step < 2 * BLOCKS:
+                multiply_second(0, step - BLOCKS)
+            if step >= BLOCKS + 2:
+                multiply_second(1, step - BLOCKS - 2)
+                hand_out(step - BLOCKS - 2)
 
-        for q in range(QUADS):
+        for q in range(QUADRANTS):
             nc.scalar.dma_start(
-                out=out_2[0, 4 * q : 4 * q + 4, :].bitcast(I32), in_=y_scales[32 * q : 32 * q + 4, :].bitcast(I32))
+                out=out_2[0, ROWS * q : ROWS * (q + 1), :].bitcast(I32),
+                in_=y_plane[32 * q : 32 * q + ROWS, :].bitcast(I32),
+            )

@@ -26,7 +26,7 @@ BLOCKS = S // TRIPS
 GROUPS = H // PASS
 LINE = 16
 PIECES = 2
-SCALAR_BLOCKS = 2
+SCALAR_BLOCKS = 1
 
 
 def tile_list_forklift_tipping_features_kernel(
@@ -49,7 +49,7 @@ def tile_list_forklift_tipping_features_kernel(
         tab_sc = held("tab_sc", 2 * T, U8)
         tab2_w = held("tab2_w", T2, U16)
         tab2_sc = held("tab2_sc", T2, U8)
-        w1_w = held("w1_w", 2 * H, U16)
+        w1_w = [held("w1_w%d" % g, 2 * PASS, U16) for g in range(GROUPS)]
         w1_sc = held("w1_sc", 2 * H, U8)
         w3_w = held("w3_w", GROUPS * N, U32)
         w3_sc = held("w3_sc", N, U8)
@@ -98,18 +98,19 @@ def tile_list_forklift_tipping_features_kernel(
         nc.sync.dma_start(idx[:], offs)
         nc.sync.dma_start(idx2[:], offs2)
         load_words(tab_w[0], tab_words[0:1].rearrange("g p c i -> g p (c i)"))
-        load_planes(tab_sc, tab_scales)
-        load_planes(tab2_sc, tab2_scales)
-        load_planes(w1_sc, w1_scales)
         load_words(tab_w[1], tab_words[1:2].rearrange("g p c i -> g p (c i)"))
+        load_planes(tab_sc, tab_scales)
+        load_planes(w1_sc, w1_scales)
+        load_planes(tab2_sc, tab2_scales)
         load_rows(w2_raw[0], w2[:, 0:PASS])
-        load_words(w1_w, w1_words)
+        load_words(w1_w[0], w1_words[:, :, 0 : 2 * PASS])
         load_words(tab2_w, tab2_words)
+        load_words(w1_w[1], w1_words[:, :, 2 * PASS : 4 * PASS])
         load_factor(gl_sb, gl)
         load_factor(gs_sb, gs)
-        load_rows(w2_raw[1], w2[:, PASS : 2 * PASS])
         load_stacked_planes(w3_sc, w3_scales)
         load_words(w3_w, w3_words.rearrange("g p c i -> g p (c i)"))
+        load_rows(w2_raw[1], w2[:, PASS : 2 * PASS])
         load_rows(w4_raw[0], w4[0:PASS, :])
         load_rows(w4_raw[1], w4[PASS : 2 * PASS, :])
 
@@ -146,15 +147,14 @@ def tile_list_forklift_tipping_features_kernel(
         w2_bf = [held("w2_bf%d" % g, PACK * PASS, BF16) for g in range(GROUPS)]
         w4_bf = [held("w4_bf%d" % g, PACK * N, BF16) for g in range(GROUPS)]
         round_and_deal(w2_bf[0], w2_raw[0], slice(0, P))
-        v_w = [gather("v_w0", U32, tab_w[0][:], idx)]
+        v_w = [gather("v_w%d" % k, U32, tab_w[k][:], idx) for k in range(2)]
         v_sc = [gather("v_sc%d" % k, U8, tab_sc[:, T * k : T * (k + 1)], idx) for k in range(2)]
-        v2_sc = gather("v2_sc", U8, tab2_sc[:], idx2)
         w1_sc_dealt = deal("w1_sc_dealt", U8, 1, by_group(w1_sc))
-        v_w.append(gather("v_w1", U32, tab_w[1][:], idx))
-        w1_w_dealt = [deal("w1_w_dealt0", U16, 2, by_group(w1_w)[:, 0::GROUPS])]
+        w1_w_dealt = [deal("w1_w_dealt0", U16, 2, by_group(w1_w[0]))]
+        v2_sc = gather("v2_sc", U8, tab2_sc[:], idx2)
         v2_w = gather("v2_w", U16, tab2_w[:], idx2)
         w2_q = [quantise("w2_0", w2_bf[0], PASS)]
-        w1_w_dealt.append(deal("w1_w_dealt1", U16, 2, by_group(w1_w)[:, 1::GROUPS]))
+        w1_w_dealt.append(deal("w1_w_dealt1", U16, 2, by_group(w1_w[1])))
         w4_q = []
 
         chunks = [(g, b) for g in range(GROUPS) for b in range(BLOCKS)]
@@ -215,7 +215,10 @@ def tile_list_forklift_tipping_features_kernel(
             nc.scalar.activation(out=sine[c][:], in_=diff[c][:], func=ACT.Sin)
 
         def make_z(c):
-            nc.vector.tensor_tensor(to_words(xz[c][:, PASS : 2 * PASS]), as_walked(sine[c]), factor(gs_sb, c), ALU.mult)
+            nc.vector.tensor_tensor(
+                xz[c][:, PASS : 2 * PASS].rearrange("p (c e t) -> p c e t", t=PACK, e=2),
+                sine[c][:].rearrange("p (c t e) -> p c e t", t=PACK, e=2),
+                factor(gs_sb, c).rearrange("p c t e -> p c e t"), ALU.mult)
 
         def quantise_chunk(c):
             xz_q[chunks[c]] = quantise("xz%d" % c, xz[c], 2 * TRIPS)
@@ -264,7 +267,7 @@ def tile_list_forklift_tipping_features_kernel(
 
         late = [("w2_1", w2_bf[1], w2_raw[1], w2_q), ("w4_0", w4_bf[0], w4_raw[0], w4_q), ("w4_1", w4_bf[1], w4_raw[1], w4_q)]
         count = len(chunks)
-        for step in range(count + 2):
+        for step in range(count + 2 + 3):
             if step < count:
                 multiply_first(step)
             if 1 <= step <= count:
@@ -274,7 +277,7 @@ def tile_list_forklift_tipping_features_kernel(
             if 1 <= step <= count:
                 make_x(step - 1)
                 take_sine(step - 1)
-            if step >= 2:
+            if 2 <= step < count + 2:
                 make_z(step - 2)
             weight, piece = divmod(step, PIECES)
             if weight < len(late):
@@ -285,13 +288,14 @@ def tile_list_forklift_tipping_features_kernel(
             if step == BLOCKS - 1:
                 w3_sc_dealt = deal("w3_sc_dealt", U8, 1, by_group(w3_sc))
                 w3_w_dealt = deal("w3_w_dealt", U32, 4, by_group(w3_w))
-            if step >= 2:
+            if 2 <= step < count + 2:
                 quantise_chunk(step - 2)
             if BLOCKS <= step < 2 * BLOCKS:
                 multiply_second(0, step - BLOCKS)
-            if step >= BLOCKS + 2:
+            if BLOCKS + 2 <= step < count + 2:
                 multiply_second(1, step - BLOCKS - 2)
-                hand_out(step - BLOCKS - 2)
+            if step >= BLOCKS + 2 + 3:
+                hand_out(step - BLOCKS - 2 - 3)
 
         for q in range(QUADRANTS):
             nc.scalar.dma_start(

@@ -58,10 +58,6 @@ def tile_list_forklift_tipping_features_kernel(
         gl_sb = held("gl_sb", GROUPS * PACK, F32)
         gs_sb = held("gs_sb", GROUPS * PACK, F32)
 
-        warm = held("warm", 16, F32)
-        nc.gpsimd.memset(warm[:, 0:1], 0.0)
-        nc.scalar.activation(out=warm[:, 8:9], in_=warm[:, 0:1], func=ACT.Silu)
-
         nc.gpsimd.memset(tab_sc[:].bitcast(I32), 0)
         nc.vector.memset(tab2_sc[:].bitcast(I32), 0)
         nc.gpsimd.memset(w1_sc[:].bitcast(I32), 0)
@@ -223,6 +219,14 @@ def tile_list_forklift_tipping_features_kernel(
         def quantise_chunk(c):
             xz_q[chunks[c]] = quantise("xz%d" % c, xz[c], 2 * TRIPS)
 
+        def quantise_half(c, half):
+            if half == 0:
+                xz_q[chunks[c]] = held("last_codes", 2 * TRIPS, U32), held("last_plane", 2 * TRIPS, U8)
+            codes, plane = xz_q[chunks[c]]
+            words = slice(TRIPS * half, TRIPS * (half + 1))
+            nc.vector.quantize_mx(
+                out=codes[:, words].bitcast(FP8X4), scales=plane[:, words], in_=xz[c][:, PASS * half : PASS * (half + 1)])
+
         y_banks = [second_psum.tile([P, PASS], F32, name="y_bank%d" % b) for b in range(BLOCKS)]
         y_codes = held("y_codes", S, U32)
         y_plane = held("y_plane", S, U8)
@@ -288,8 +292,10 @@ def tile_list_forklift_tipping_features_kernel(
             if step == BLOCKS - 1:
                 w3_sc_dealt = deal("w3_sc_dealt", U8, 1, by_group(w3_sc))
                 w3_w_dealt = deal("w3_w_dealt", U32, 4, by_group(w3_w))
-            if 2 <= step < count + 2:
+            if 2 <= step <= count:
                 quantise_chunk(step - 2)
+            if count <= step < count + 2:
+                quantise_half(count - 1, step - count)
             if BLOCKS <= step < 2 * BLOCKS:
                 multiply_second(0, step - BLOCKS)
             if BLOCKS + 2 <= step < count + 2:

@@ -24,9 +24,12 @@ ROWS = 4
 TRIPS = 128
 BLOCKS = S // TRIPS
 GROUPS = H // PASS
+LIFT = S + H + N
+KIB = 1024
+HALF = PASS // 2
 LINE = 16
-PIECES = 2
-SCALAR_BLOCKS = 1
+PIECES = 4
+SCALAR_BLOCKS = 3
 
 
 def tile_list_forklift_tipping_features_kernel(
@@ -37,7 +40,7 @@ def tile_list_forklift_tipping_features_kernel(
     with ExitStack() as ctx:
         keep = ctx.enter_context(tc.tile_pool(name="keep", bufs=1))
         work = ctx.enter_context(tc.tile_pool(name="work", bufs=3))
-        first_psum = ctx.enter_context(tc.psum_pool(name="first_psum", bufs=2))
+        first_psum = ctx.enter_context(tc.psum_pool(name="first_psum", bufs=1))
         second_psum = ctx.enter_context(tc.psum_pool(name="second_psum", bufs=1))
 
         def held(name, columns, dtype):
@@ -46,22 +49,27 @@ def tile_list_forklift_tipping_features_kernel(
         idx = keep.tile([P, S // 16], U16, name="idx")
         idx2 = keep.tile([P, S // 16], U16, name="idx2")
         tab_w = [held("tab_w%d" % k, T, U32) for k in range(2)]
-        tab_sc = held("tab_sc", 2 * T, U8)
         tab2_w = held("tab2_w", T2, U16)
-        tab2_sc = held("tab2_sc", T2, U8)
         w1_w = [held("w1_w%d" % g, 2 * PASS, U16) for g in range(GROUPS)]
-        w1_sc = held("w1_sc", 2 * H, U8)
         w3_w = held("w3_w", GROUPS * N, U32)
-        w3_sc = held("w3_sc", N, U8)
-        w2_raw = [held("w2_raw%d" % g, PACK * PASS, F32) for g in range(GROUPS)]
-        w4_raw = [held("w4_raw%d" % g, PACK * N, F32) for g in range(GROUPS)]
         gl_sb = held("gl_sb", GROUPS * PACK, F32)
         gs_sb = held("gs_sb", GROUPS * PACK, F32)
+        v_rows = held("v_rows", S, U8)
+        tab2_rows = held("tab2_rows", T2, U8)
+        staged = ctx.enter_context(tc.tile_pool(name="staged", bufs=1))
+        raw = [staged.tile([P, PACK * HALF], F32, name="raw%d" % h, offset=4 * KIB * h) for h in range(8)]
 
-        nc.gpsimd.memset(tab_sc[:].bitcast(I32), 0)
-        nc.vector.memset(tab2_sc[:].bitcast(I32), 0)
-        nc.gpsimd.memset(w1_sc[:].bitcast(I32), 0)
-        nc.gpsimd.memset(w3_sc[:].bitcast(I32), 0)
+        tab_rows = held("tab_rows", T, U8)
+        w_rows = held("w_rows", H + N, U8)
+        lift = held("lift", LIFT, U8)
+        planes = held("planes", 2 * LIFT, U8)
+        v2_sc = held("v2_sc", S, U8)
+
+        nc.vector.memset(tab_rows[0:96, :].bitcast(I32), 0)
+        nc.vector.memset(w_rows[0:96, :].bitcast(I32), 0)
+        nc.vector.memset(tab2_rows[0:112, :].bitcast(I32), 0)
+        nc.gpsimd.memset(planes[:].bitcast(I32), 0)
+        nc.vector.memset(v2_sc[:].bitcast(I32), 0)
 
         def load_words(tile, words):
             nc.sync.dma_start(
@@ -69,19 +77,8 @@ def tile_list_forklift_tipping_features_kernel(
                 in_=words.bitcast(I32).rearrange("g p c -> p g c"),
             )
 
-        def load_planes(tile, scales):
-            for q in range(QUADRANTS):
-                nc.sync.dma_start(
-                    out=tile[32 * q : 32 * q + ROWS, :].bitcast(I32).rearrange("r (g c) -> r g c", g=scales.shape[0]),
-                    in_=scales[:, ROWS * q : ROWS * (q + 1), :].bitcast(I32).rearrange("g r c -> r g c"),
-                )
-
-        def load_stacked_planes(tile, scales):
-            for q in range(QUADRANTS):
-                nc.sync.dma_start(
-                    out=tile[32 * q : 32 * q + GROUPS * ROWS, :].bitcast(I32),
-                    in_=scales[:, ROWS * q : ROWS * (q + 1), :].bitcast(I32),
-                )
+        def load_scale_rows(rows, scales):
+            nc.sync.dma_start(out=rows.bitcast(I32), in_=scales.bitcast(I32).rearrange("a q c -> q a c"))
 
         def load_rows(tile, rows):
             nc.sync.dma_start(
@@ -92,46 +89,37 @@ def tile_list_forklift_tipping_features_kernel(
                 out=tile[:].rearrange("p (g t) -> p g t", t=PACK), in_=factor.rearrange("(g p t) -> p g t", p=P, t=PACK))
 
         nc.sync.dma_start(idx[:], offs)
+        load_scale_rows(tab_rows[96:P, :], tab_scales)
+        load_scale_rows(w_rows[96:P, 0:H], w1_scales)
+        load_scale_rows(w_rows[96:P, H : H + N], w3_scales)
         nc.sync.dma_start(idx2[:], offs2)
+        load_scale_rows(tab2_rows[112:P, :], tab2_scales)
         load_words(tab_w[0], tab_words[0:1].rearrange("g p c i -> g p (c i)"))
-        load_words(tab_w[1], tab_words[1:2].rearrange("g p c i -> g p (c i)"))
-        load_planes(tab_sc, tab_scales)
-        load_planes(w1_sc, w1_scales)
-        load_planes(tab2_sc, tab2_scales)
-        load_rows(w2_raw[0], w2[:, 0:PASS])
+        load_rows(raw[0], w2[:, 0:HALF])
         load_words(w1_w[0], w1_words[:, :, 0 : 2 * PASS])
-        load_words(tab2_w, tab2_words)
-        load_words(w1_w[1], w1_words[:, :, 2 * PASS : 4 * PASS])
-        load_factor(gl_sb, gl)
-        load_factor(gs_sb, gs)
-        load_stacked_planes(w3_sc, w3_scales)
-        load_words(w3_w, w3_words.rearrange("g p c i -> g p (c i)"))
-        load_rows(w2_raw[1], w2[:, PASS : 2 * PASS])
-        load_rows(w4_raw[0], w4[0:PASS, :])
-        load_rows(w4_raw[1], w4[PASS : 2 * PASS, :])
+        load_words(tab_w[1], tab_words[1:2].rearrange("g p c i -> g p (c i)"))
+        load_rows(raw[1], w2[:, HALF:PASS])
 
         def gather(name, dtype, window, offsets):
             picked = held(name, S, dtype)
             nc.vector.tensor_copy(picked[:], window.indirect(offsets[:]))
             return picked
 
-        def deal(name, dtype, size, packed):
+        def deal(dealt, size, packed):
             run = LINE // size
             groups = packed.shape[1]
-            dealt = held(name, groups * PASS, dtype)
             nc.vector.tensor_copy(
-                out=dealt[:].rearrange("p (g t c u) -> p g c t u", g=groups, t=PACK, u=run),
-                in_=packed.rearrange("p g (c u t) -> p g c t u", t=PACK, u=run),
+                out=dealt.rearrange("p (g t c u) -> p c g t u", g=groups, t=PACK, u=run),
+                in_=packed.rearrange("p g (c u t) -> p c g t u", t=PACK, u=run),
             )
-            return dealt
 
         def by_group(tile):
             return tile[:].rearrange("p (g c) -> p g c", c=PASS)
 
-        def round_and_deal(rounded, raw, part):
+        def round_and_deal(rounded, raw, part, raw_part):
             nc.scalar.copy(
                 out=rounded[:].rearrange("p (s e m i) -> p s m i e", s=2, e=2, i=PACK)[:, :, part],
-                in_=raw[:].rearrange("p (i m s e) -> p s m i e", i=PACK, s=2, e=2)[:, :, part],
+                in_=raw[:].rearrange("p (i m s e) -> p s m i e", i=PACK, s=2, e=2)[:, :, raw_part],
             )
 
         def quantise(name, values, columns):
@@ -142,15 +130,40 @@ def tile_list_forklift_tipping_features_kernel(
 
         w2_bf = [held("w2_bf%d" % g, PACK * PASS, BF16) for g in range(GROUPS)]
         w4_bf = [held("w4_bf%d" % g, PACK * N, BF16) for g in range(GROUPS)]
-        round_and_deal(w2_bf[0], w2_raw[0], slice(0, P))
+        for h in range(2):
+            round_and_deal(w2_bf[0], raw[h], slice(P // 2 * h, P // 2 * (h + 1)), slice(0, P // 2))
+
+        nc.vector.tensor_copy(v_rows[:], tab_rows[:].indirect(idx[:]))
+        deal(lift[:, S:LIFT], 1, by_group(w_rows))
+        nc.vector.tensor_copy(lift[:, 0:S].bitcast(I32), v_rows[:].bitcast(I32))
+        for q in range(QUADRANTS):
+            nc.sync.dma_start(
+                out=planes[32 * q : 32 * q + ROWS, :].bitcast(I32).rearrange("r (a c) -> r a c", a=2),
+                in_=lift[96 + 2 * ROWS * q : 96 + 2 * ROWS * (q + 1), :].bitcast(I32))
+        load_words(tab2_w, tab2_words)
+        v2_rows = gather("v2_rows", U8, tab2_rows[:], idx2)
+        for q in range(QUADRANTS):
+            nc.sync.dma_start(
+                out=v2_sc[32 * q : 32 * q + ROWS, :].bitcast(I32),
+                in_=v2_rows[112 + ROWS * q : 112 + ROWS * (q + 1), :].bitcast(I32))
+        load_factor(gl_sb, gl)
+        load_factor(gs_sb, gs)
         v_w = [gather("v_w%d" % k, U32, tab_w[k][:], idx) for k in range(2)]
-        v_sc = [gather("v_sc%d" % k, U8, tab_sc[:, T * k : T * (k + 1)], idx) for k in range(2)]
-        w1_sc_dealt = deal("w1_sc_dealt", U8, 1, by_group(w1_sc))
-        w1_w_dealt = [deal("w1_w_dealt0", U16, 2, by_group(w1_w[0]))]
-        v2_sc = gather("v2_sc", U8, tab2_sc[:], idx2)
-        v2_w = gather("v2_w", U16, tab2_w[:], idx2)
+        w1_w_dealt = [held("w1_w_dealt%d" % g, 2 * PASS, U16) for g in range(GROUPS)]
+        deal(w1_w_dealt[0][:], 2, by_group(w1_w[0]))
         w2_q = [quantise("w2_0", w2_bf[0], PASS)]
-        w1_w_dealt.append(deal("w1_w_dealt1", U16, 2, by_group(w1_w[1])))
+        v2_w = held("v2_w", S, U16)
+        for h in range(2):
+            nc.vector.tensor_copy(
+                v2_w[:, S // 2 * h : S // 2 * (h + 1)], tab2_w[:].indirect(idx2[:, S // 32 * h : S // 32 * (h + 1)]))
+        load_rows(raw[2], w2[:, PASS : PASS + HALF])
+        load_rows(raw[3], w2[:, PASS + HALF : 2 * PASS])
+        load_words(w1_w[1], w1_words[:, :, 2 * PASS : 4 * PASS])
+        load_rows(raw[4], w4[0:PASS, 0:HALF])
+        load_rows(raw[5], w4[0:PASS, HALF:N])
+        load_words(w3_w, w3_words.rearrange("g p c i -> g p (c i)"))
+        load_rows(raw[6], w4[PASS : 2 * PASS, 0:HALF])
+        load_rows(raw[7], w4[PASS : 2 * PASS, HALF:N])
         w4_q = []
 
         chunks = [(g, b) for g in range(GROUPS) for b in range(BLOCKS)]
@@ -172,16 +185,17 @@ def tile_list_forklift_tipping_features_kernel(
         def multiply_first(c):
             g, b = chunks[c]
             trips = slice(TRIPS * b, TRIPS * (b + 1))
-            a_bank = first_psum.tile([P, PASS], F32, name="a_bank")
-            load_bank = first_psum.tile([P, PASS], F32, name="load_bank")
+            swap = 0 if c < 2 else 1
+            a_bank = first_psum.tile([P, PASS], F32, name="a_bank", tag="bank%d" % (2 * (c % 2) + swap))
+            load_bank = first_psum.tile([P, PASS], F32, name="load_bank", tag="bank%d" % (2 * (c % 2) + 1 - swap))
             for t in range(PACK):
                 for k in range(2):
-                    first = H * k + PASS * g + P * t
+                    first = LIFT * k + S + PASS * g + P * t
                     nc.tensor.matmul_mx(
                         out=a_bank[:, TRIPS * t : TRIPS * (t + 1)],
                         lhsT=w1_w_dealt[g][:, PASS * k + P * t : PASS * k + P * (t + 1)].bitcast(FP4X4),
-                        lhsT_scale=w1_sc_dealt[:, first : first + P],
-                        rhs=v_w[k][:, trips].bitcast(FP8X4), rhs_scale=v_sc[k][:, trips],
+                        lhsT_scale=planes[:, first : first + P],
+                        rhs=v_w[k][:, trips].bitcast(FP8X4), rhs_scale=planes[:, LIFT * k + TRIPS * b : LIFT * k + TRIPS * (b + 1)],
                         start=(k == 0), stop=(k == 1),
                     )
             codes, plane = w2_q[g]
@@ -195,7 +209,8 @@ def tile_list_forklift_tipping_features_kernel(
             banks[c] = a_bank, load_bank
 
         def gate(c):
-            gated[c] = work.tile([P, PASS], F32, name="gated")
+            at = 4 * KIB * c if c >= 2 else 4 * KIB + 2 * KIB * c
+            gated[c] = staged.tile([P, PASS], F32, name="gated%d" % c, offset=at)
             nc.scalar.activation(out=as_walked(gated[c]), in_=from_bank(banks[c][0]), func=ACT.Silu)
 
         def subtract(c):
@@ -207,7 +222,8 @@ def tile_list_forklift_tipping_features_kernel(
             nc.vector.tensor_tensor(to_words(xz[c][:, 0:PASS]), from_bank(banks[c][1]), factor(gl_sb, c), ALU.mult)
 
         def take_sine(c):
-            sine[c] = work.tile([P, PASS], F32, name="sine")
+            at = 4 * KIB * (c + 2) + 2 * KIB if c < 6 else 2 * KIB * (c - 6)
+            sine[c] = staged.tile([P, PASS], F32, name="sine%d" % c, offset=at)
             nc.scalar.activation(out=sine[c][:], in_=diff[c][:], func=ACT.Sin)
 
         def make_z(c):
@@ -237,7 +253,7 @@ def tile_list_forklift_tipping_features_kernel(
                 nc.tensor.matmul_mx(
                     out=y_banks[b][:, TRIPS * t : TRIPS * (t + 1)],
                     lhsT=w3_w_dealt[:, N * g + P * t : N * g + P * (t + 1)].bitcast(FP8X4),
-                    lhsT_scale=w3_sc_dealt[ROWS * g : P, P * t : P * (t + 1)],
+                    lhsT_scale=planes[:, LIFT * g + S + H + P * t : LIFT * g + S + H + P * (t + 1)],
                     rhs=codes[:, 0:TRIPS].bitcast(FP8X4), rhs_scale=plane[:, 0:TRIPS],
                     start=(g == 0 and t == 0), stop=False,
                 )
@@ -269,39 +285,45 @@ def tile_list_forklift_tipping_features_kernel(
                 nc.sync.dma_start(
                     out=out_1[0].rearrange("p m t -> p (m t)").bitcast(I32)[:, pair], in_=y_codes[:, pair].bitcast(I32))
 
-        late = [("w2_1", w2_bf[1], w2_raw[1], w2_q), ("w4_0", w4_bf[0], w4_raw[0], w4_q), ("w4_1", w4_bf[1], w4_raw[1], w4_q)]
+        late = [("w2_1", w2_bf[1], w2_q), ("w4_0", w4_bf[0], w4_q), ("w4_1", w4_bf[1], w4_q)]
         count = len(chunks)
-        for step in range(count + 2 + 3):
+        w3_w_dealt = held("w3_w_dealt", GROUPS * N, U32)
+        for step in range(count + 2):
             if step < count:
                 multiply_first(step)
-            if 1 <= step <= count:
-                subtract(step - 1)
-            if step < count:
                 gate(step)
             if 1 <= step <= count:
-                make_x(step - 1)
+                subtract(step - 1)
                 take_sine(step - 1)
             if 2 <= step < count + 2:
                 make_z(step - 2)
-            weight, piece = divmod(step, PIECES)
-            if weight < len(late):
-                round_and_deal(late[weight][1], late[weight][2], slice(P // PIECES * piece, P // PIECES * (piece + 1)))
-            if piece == 0 and 1 <= weight <= len(late):
-                name, rounded, raw, quantised = late[weight - 1]
-                quantised.append(quantise(name, rounded, PASS))
-            if step == BLOCKS - 1:
-                w3_sc_dealt = deal("w3_sc_dealt", U8, 1, by_group(w3_sc))
-                w3_w_dealt = deal("w3_w_dealt", U32, 4, by_group(w3_w))
+            if 1 <= step <= count:
+                make_x(step - 1)
             if 2 <= step <= count:
                 quantise_chunk(step - 2)
             if count <= step < count + 2:
                 quantise_half(count - 1, step - count)
-            if BLOCKS <= step < 2 * BLOCKS:
-                multiply_second(0, step - BLOCKS)
-            if BLOCKS + 2 <= step < count + 2:
-                multiply_second(1, step - BLOCKS - 2)
-            if step >= BLOCKS + 2 + 3:
-                hand_out(step - BLOCKS - 2 - 3)
+            weight, half = divmod(step, 2)
+            if 0 <= weight < len(late):
+                for piece in range(PIECES // 2 * half, PIECES // 2 * (half + 1)):
+                    width = P // PIECES
+                    inside = piece - PIECES // 2 * half
+                    round_and_deal(
+                        late[weight][1], raw[2 + 2 * weight + half],
+                        slice(width * piece, width * (piece + 1)), slice(width * inside, width * (inside + 1)))
+            if half == 0 and 1 <= weight <= len(late):
+                name, rounded, quantised = late[weight - 1]
+                quantised.append(quantise(name, rounded, PASS))
+            if step == 2:
+                deal(w1_w_dealt[1][:], 2, by_group(w1_w[1]))
+            if step == 4:
+                deal(w3_w_dealt[:], 4, by_group(w3_w))
+            if 4 <= step < 6:
+                multiply_second(0, 2 * (step - 4))
+                multiply_second(0, 2 * (step - 4) + 1)
+            if 6 <= step < count + 2:
+                multiply_second(1, step - 6)
+                hand_out(step - 6)
 
         for q in range(QUADRANTS):
             nc.scalar.dma_start(

@@ -28,8 +28,8 @@ LIFT = S + H + N
 KIB = 1024
 HALF = PASS // 2
 LINE = 16
-PIECES = 4
-SCALAR_BLOCKS = 3
+PIECES = 2
+SCALAR_BLOCKS = 1
 
 
 def tile_list_forklift_tipping_features_kernel(

@@ -172,9 +172,6 @@ def tile_list_forklift_tipping_features_kernel(
         def from_bank(bank):
             return bank[:].rearrange("p (t c e) -> p c t e", t=PACK, e=2)
 
-        def as_walked(tile):
-            return tile[:].rearrange("p (c t e) -> p c t e", t=PACK, e=2)
-
         def to_words(columns):
             return columns.rearrange("p (c e t) -> p c t e", t=PACK, e=2)
 
@@ -211,11 +208,11 @@ def tile_list_forklift_tipping_features_kernel(
         def gate(c):
             at = 4 * KIB * c if c >= 2 else 4 * KIB + 2 * KIB * c
             gated[c] = staged.tile([P, PASS], F32, name="gated%d" % c, offset=at)
-            nc.scalar.activation(out=as_walked(gated[c]), in_=from_bank(banks[c][0]), func=ACT.Silu)
+            nc.scalar.activation(out=gated[c][:], in_=banks[c][0][:], func=ACT.Silu)
 
         def subtract(c):
             diff[c] = work.tile([P, PASS], F32, name="diff")
-            nc.vector.tensor_tensor(as_walked(diff[c]), as_walked(gated[c]), from_bank(banks[c][1]), ALU.subtract)
+            nc.vector.tensor_tensor(diff[c][:], gated[c][:], banks[c][1][:], ALU.subtract)
 
         def make_x(c):
             xz[c] = work.tile([P, 2 * PASS], BF16, name="xz", align_bytes=64, bufs=4)
@@ -227,10 +224,12 @@ def tile_list_forklift_tipping_features_kernel(
             nc.scalar.activation(out=sine[c][:], in_=diff[c][:], func=ACT.Sin)
 
         def make_z(c):
+            g = chunks[c][0]
             nc.vector.tensor_tensor(
-                xz[c][:, PASS : 2 * PASS].rearrange("p (c e t) -> p c e t", t=PACK, e=2),
-                sine[c][:].rearrange("p (c t e) -> p c e t", t=PACK, e=2),
-                factor(gs_sb, c).rearrange("p c t e -> p c e t"), ALU.mult)
+                xz[c][:, PASS : 2 * PASS].rearrange("p (c e t) -> p c t e", t=PACK, e=4),
+                sine[c][:].rearrange("p (t c e) -> p c t e", t=PACK, e=4),
+                gs_sb[:, PACK * g : PACK * (g + 1)].unsqueeze(1).unsqueeze(3).to_broadcast([P, TRIPS // 4, PACK, 4]),
+                ALU.mult)
 
         def quantise_chunk(c):
             xz_q[chunks[c]] = quantise("xz%d" % c, xz[c], 2 * TRIPS)
@@ -266,24 +265,32 @@ def tile_list_forklift_tipping_features_kernel(
                     start=False, stop=(g == GROUPS - 1 and t == PACK - 1),
                 )
 
-        def hand_out(b):
-            trips = slice(TRIPS * b, TRIPS * (b + 1))
-            y = held("y%d" % b, PACK * TRIPS, F32)
-            nc.scalar.copy(out=y[:], in_=y_banks[b][:])
+        y = [held("y%d" % b, PACK * TRIPS, F32) for b in range(BLOCKS)]
+        y_bf = held("y_bf", PACK * S, BF16)
+
+        def store_y(b):
+            nc.scalar.copy(out=y[b][:], in_=y_banks[b][:])
             nc.sync.dma_start(
-                out=out_0.rearrange("(p t) j -> p t j", t=PACK)[:, :, trips],
-                in_=y[:].rearrange("p (t j) -> p t j", t=PACK),
+                out=out_0.rearrange("(p t) j -> p t j", t=PACK)[:, :, TRIPS * b : TRIPS * (b + 1)],
+                in_=y[b][:].rearrange("p (t j) -> p t j", t=PACK),
             )
-            y_bf = held("y_bf%d" % b, PACK * TRIPS, BF16)
+
+        def round_y(b):
+            rounded = to_words(y_bf[:, PASS * b : PASS * (b + 1)])
             if b < SCALAR_BLOCKS:
-                nc.scalar.copy(out=to_words(y_bf[:]), in_=from_bank(y_banks[b]))
+                nc.scalar.copy(out=rounded, in_=from_bank(y_banks[b]))
             else:
-                nc.vector.tensor_copy(out=to_words(y_bf[:]), in_=from_bank(y))
-            nc.vector.quantize_mx(out=y_codes[:, trips].bitcast(FP8X4), scales=y_plane[:, trips], in_=y_bf[:])
-            if b % 2 == 1:
-                pair = slice(TRIPS * (b - 1), TRIPS * (b + 1))
-                nc.sync.dma_start(
-                    out=out_1[0].rearrange("p m t -> p (m t)").bitcast(I32)[:, pair], in_=y_codes[:, pair].bitcast(I32))
+                nc.vector.tensor_copy(out=rounded, in_=from_bank(y[b]))
+
+        def quantise_y(first, last):
+            trips = slice(TRIPS * first, TRIPS * last)
+            nc.vector.quantize_mx(
+                out=y_codes[:, trips].bitcast(FP8X4), scales=y_plane[:, trips], in_=y_bf[:, PASS * first : PASS * last])
+
+        def store_codes(first, last):
+            trips = slice(TRIPS * first, TRIPS * last)
+            nc.sync.dma_start(
+                out=out_1[0].rearrange("p m t -> p (m t)").bitcast(I32)[:, trips], in_=y_codes[:, trips].bitcast(I32))
 
         late = [("w2_1", w2_bf[1], w2_q), ("w4_0", w4_bf[0], w4_q), ("w4_1", w4_bf[1], w4_q)]
         count = len(chunks)
@@ -323,7 +330,18 @@ def tile_list_forklift_tipping_features_kernel(
                 multiply_second(0, 2 * (step - 4) + 1)
             if 6 <= step < count + 2:
                 multiply_second(1, step - 6)
-                hand_out(step - 6)
+                store_y(step - 6)
+            if step == 6:
+                round_y(0)
+
+        round_y(1)
+        round_y(2)
+        quantise_y(0, 2)
+        quantise_y(2, 3)
+        store_codes(0, 3)
+        round_y(3)
+        quantise_y(3, 4)
+        store_codes(3, 4)
 
         for q in range(QUADRANTS):
             nc.scalar.dma_start(

@@ -71,6 +71,10 @@ def tile_list_forklift_tipping_features_kernel(
         nc.gpsimd.memset(planes[:].bitcast(I32), 0)
         nc.vector.memset(v2_sc[:].bitcast(I32), 0)
 
+        warm = held("warm", 16, F32)
+        nc.gpsimd.memset(warm[:, 0:1], 0.0)
+        nc.scalar.activation(out=warm[:, 8:9], in_=warm[:, 0:1], func=ACT.Silu)
+
         def load_words(tile, words):
             nc.sync.dma_start(
                 out=tile[:].bitcast(I32).rearrange("p (g c) -> p g c", g=words.shape[0]),

@@ -120,8 +120,8 @@ def tile_list_forklift_tipping_features_kernel(
         def by_group(tile):
             return tile[:].rearrange("p (g c) -> p g c", c=PASS)
 
-        def round_and_deal(rounded, raw, part, raw_part):
-            nc.scalar.copy(
+        def round_and_deal(rounded, raw, part, raw_part, copy=nc.scalar.copy):
+            copy(
                 out=rounded[:].rearrange("p (s e m i) -> p s m i e", s=2, e=2, i=PACK)[:, :, part],
                 in_=raw[:].rearrange("p (i m s e) -> p s m i e", i=PACK, s=2, e=2)[:, :, raw_part],
             )
@@ -216,10 +216,10 @@ def tile_list_forklift_tipping_features_kernel(
 
         def subtract(c):
             diff[c] = work.tile([P, PASS], F32, name="diff")
-            nc.vector.tensor_tensor(diff[c][:], gated[c][:], banks[c][1][:], ALU.subtract)
+            nc.vector.tensor_tensor(to_words(diff[c][:]), from_bank(gated[c]), from_bank(banks[c][1]), ALU.subtract)
 
         def make_x(c):
-            xz[c] = work.tile([P, 2 * PASS], BF16, name="xz", align_bytes=64, bufs=4)
+            xz[c] = work.tile([P, 2 * PASS], BF16, name="xz", align_bytes=64, bufs=5)
             nc.vector.tensor_tensor(to_words(xz[c][:, 0:PASS]), from_bank(banks[c][1]), factor(gl_sb, c), ALU.mult)
 
         def take_sine(c):
@@ -229,11 +229,11 @@ def tile_list_forklift_tipping_features_kernel(
 
         def make_z(c):
             g = chunks[c][0]
-            nc.vector.tensor_tensor(
-                xz[c][:, PASS : 2 * PASS].rearrange("p (c e t) -> p c t e", t=PACK, e=4),
-                sine[c][:].rearrange("p (t c e) -> p c t e", t=PACK, e=4),
-                gs_sb[:, PACK * g : PACK * (g + 1)].unsqueeze(1).unsqueeze(3).to_broadcast([P, TRIPS // 4, PACK, 4]),
-                ALU.mult)
+            engine = nc.gpsimd if c < count - 1 else nc.vector
+            engine.tensor_tensor(
+                xz[c][:, PASS : 2 * PASS].rearrange("p (j t) -> p j t", t=PACK),
+                sine[c][:].rearrange("p (j t) -> p j t", t=PACK),
+                gs_sb[:, PACK * g : PACK * (g + 1)].unsqueeze(1).to_broadcast([P, TRIPS, PACK]), ALU.mult)
 
         def quantise_chunk(c):
             xz_q[chunks[c]] = quantise("xz%d" % c, xz[c], 2 * TRIPS)
@@ -310,8 +310,8 @@ def tile_list_forklift_tipping_features_kernel(
                 make_z(step - 2)
             if 1 <= step <= count:
                 make_x(step - 1)
-            if 2 <= step <= count:
-                quantise_chunk(step - 2)
+            if 3 <= step < count + 2:
+                quantise_chunk(step - 3)
             if count <= step < count + 2:
                 quantise_half(count - 1, step - count)
             weight, half = divmod(step, 2)
@@ -321,7 +321,8 @@ def tile_list_forklift_tipping_features_kernel(
                     inside = piece - PIECES // 2 * half
                     round_and_deal(
                         late[weight][1], raw[2 + 2 * weight + half],
-                        slice(width * piece, width * (piece + 1)), slice(width * inside, width * (inside + 1)))
+                        slice(width * piece, width * (piece + 1)), slice(width * inside, width * (inside + 1)),
+                        nc.vector.tensor_copy if half == 1 else nc.scalar.copy)
             if half == 0 and 1 <= weight <= len(late):
                 name, rounded, quantised = late[weight - 1]
                 quantised.append(quantise(name, rounded, PASS))
@@ -329,14 +330,16 @@ def tile_list_forklift_tipping_features_kernel(
                 deal(w1_w_dealt[1][:], 2, by_group(w1_w[1]))
             if step == 4:
                 deal(w3_w_dealt[:], 4, by_group(w3_w))
-            if 4 <= step < 6:
-                multiply_second(0, 2 * (step - 4))
-                multiply_second(0, 2 * (step - 4) + 1)
-            if 6 <= step < count + 2:
-                multiply_second(1, step - 6)
-                store_y(step - 6)
-            if step == 6:
+            if 5 <= step < 7:
+                multiply_second(0, 2 * (step - 5))
+                multiply_second(0, 2 * (step - 5) + 1)
+            if 7 <= step < count + 2:
+                multiply_second(1, step - 7)
+                store_y(step - 7)
+            if step == 7:
                 round_y(0)
+        multiply_second(1, 3)
+        store_y(3)
 
         round_y(1)
         round_y(2)

@@ -120,8 +120,8 @@ def tile_list_forklift_tipping_features_kernel(
         def by_group(tile):
             return tile[:].rearrange("p (g c) -> p g c", c=PASS)
 
-        def round_and_deal(rounded, raw, part, raw_part, copy=nc.scalar.copy):
-            copy(
+        def round_and_deal(rounded, raw, part, raw_part):
+            nc.scalar.copy(
                 out=rounded[:].rearrange("p (s e m i) -> p s m i e", s=2, e=2, i=PACK)[:, :, part],
                 in_=raw[:].rearrange("p (i m s e) -> p s m i e", i=PACK, s=2, e=2)[:, :, raw_part],
             )
@@ -321,8 +321,7 @@ def tile_list_forklift_tipping_features_kernel(
                     inside = piece - PIECES // 2 * half
                     round_and_deal(
                         late[weight][1], raw[2 + 2 * weight + half],
-                        slice(width * piece, width * (piece + 1)), slice(width * inside, width * (inside + 1)),
-                        nc.vector.tensor_copy if half == 1 else nc.scalar.copy)
+                        slice(width * piece, width * (piece + 1)), slice(width * inside, width * (inside + 1)))
             if half == 0 and 1 <= weight <= len(late):
                 name, rounded, quantised = late[weight - 1]
                 quantised.append(quantise(name, rounded, PASS))

@@ -126,6 +126,12 @@ def tile_list_forklift_tipping_features_kernel(
                 in_=raw[:].rearrange("p (i m s e) -> p s m i e", i=PACK, s=2, e=2)[:, :, raw_part],
             )
 
+        def round_and_deal_on_vector(rounded, raw, half):
+            nc.vector.tensor_copy(
+                out=rounded[:].rearrange("p (t h u m i) -> p h u t m i", t=PACK, h=2, u=2, i=PACK)[:, half],
+                in_=raw[:].rearrange("p (i u m t) -> p u t m i", i=PACK, u=2, t=PACK),
+            )
+
         def quantise(name, values, columns):
             codes = held(name + "_codes", columns, U32)
             plane = held(name + "_plane", columns, U8)
@@ -315,7 +321,9 @@ def tile_list_forklift_tipping_features_kernel(
             if count <= step < count + 2:
                 quantise_half(count - 1, step - count)
             weight, half = divmod(step, 2)
-            if 0 <= weight < len(late):
+            if step in (1, 3):
+                round_and_deal_on_vector(late[weight][1], raw[2 + step], half)
+            elif 0 <= weight < len(late):
                 for piece in range(PIECES // 2 * half, PIECES // 2 * (half + 1)):
                     width = P // PIECES
                     inside = piece - PIECES // 2 * half

@@ -29,7 +29,7 @@ KIB = 1024
 HALF = PASS // 2
 LINE = 16
 PIECES = 2
-SCALAR_BLOCKS = 1
+SCALAR_BLOCKS = 0
 
 
 def tile_list_forklift_tipping_features_kernel(
@@ -120,16 +120,10 @@ def tile_list_forklift_tipping_features_kernel(
         def by_group(tile):
             return tile[:].rearrange("p (g c) -> p g c", c=PASS)
 
-        def round_and_deal(rounded, raw, part, raw_part):
-            nc.scalar.copy(
+        def round_and_deal(rounded, raw, part, raw_part, copy=nc.scalar.copy):
+            copy(
                 out=rounded[:].rearrange("p (s e m i) -> p s m i e", s=2, e=2, i=PACK)[:, :, part],
                 in_=raw[:].rearrange("p (i m s e) -> p s m i e", i=PACK, s=2, e=2)[:, :, raw_part],
-            )
-
-        def round_and_deal_on_vector(rounded, raw, half):
-            nc.vector.tensor_copy(
-                out=rounded[:].rearrange("p (t h u m i) -> p h u t m i", t=PACK, h=2, u=2, i=PACK)[:, half],
-                in_=raw[:].rearrange("p (i u m t) -> p u t m i", i=PACK, u=2, t=PACK),
             )
 
         def quantise(name, values, columns):
@@ -158,9 +152,12 @@ def tile_list_forklift_tipping_features_kernel(
                 in_=v2_rows[112 + ROWS * q : 112 + ROWS * (q + 1), :].bitcast(I32))
         load_factor(gl_sb, gl)
         load_factor(gs_sb, gs)
-        v_w = [gather("v_w%d" % k, U32, tab_w[k][:], idx) for k in range(2)]
+        v_w = [gather("v_w0", U32, tab_w[0][:], idx), held("v_w1", S, U32)]
         w1_w_dealt = [held("w1_w_dealt%d" % g, 2 * PASS, U16) for g in range(GROUPS)]
         deal(w1_w_dealt[0][:], 2, by_group(w1_w[0]))
+        for h in range(2):
+            nc.vector.tensor_copy(
+                v_w[1][:, S // 2 * h : S // 2 * (h + 1)], tab_w[1][:].indirect(idx[:, S // 32 * h : S // 32 * (h + 1)]))
         w2_q = [quantise("w2_0", w2_bf[0], PASS)]
         v2_w = held("v2_w", S, U16)
         for h in range(2):
@@ -321,15 +318,14 @@ def tile_list_forklift_tipping_features_kernel(
             if count <= step < count + 2:
                 quantise_half(count - 1, step - count)
             weight, half = divmod(step, 2)
-            if step in (1, 3):
-                round_and_deal_on_vector(late[weight][1], raw[2 + step], half)
-            elif 0 <= weight < len(late):
+            if 0 <= weight < len(late):
                 for piece in range(PIECES // 2 * half, PIECES // 2 * (half + 1)):
                     width = P // PIECES
                     inside = piece - PIECES // 2 * half
                     round_and_deal(
                         late[weight][1], raw[2 + 2 * weight + half],
-                        slice(width * piece, width * (piece + 1)), slice(width * inside, width * (inside + 1)))
+                        slice(width * piece, width * (piece + 1)), slice(width * inside, width * (inside + 1)),
+                        nc.vector.tensor_copy if step == 3 else nc.scalar.copy)
             if half == 0 and 1 <= weight <= len(late):
                 name, rounded, quantised = late[weight - 1]
                 quantised.append(quantise(name, rounded, PASS))
@@ -343,11 +339,10 @@ def tile_list_forklift_tipping_features_kernel(
             if 7 <= step < count + 2:
                 multiply_second(1, step - 7)
                 store_y(step - 7)
-            if step == 7:
-                round_y(0)
         multiply_second(1, 3)
         store_y(3)
 
+        round_y(0)
         round_y(1)
         round_y(2)
         quantise_y(0, 2)

@@ -184,7 +184,13 @@ def tile_list_forklift_tipping_features_kernel(
 
         def factor(tile, c):
             g = chunks[c][0]
-            return tile[:, PACK * g : PACK * (g + 1)].unsqueeze(1).unsqueeze(3).to_broadcast([P, TRIPS // 2, PACK, 2])
+            return tile[:, PACK * g : PACK * (g + 1)].unsqueeze(1).to_broadcast([P, TRIPS, PACK])
+
+        def across(bank):
+            return bank[:].rearrange("p (t j) -> p j t", t=PACK)
+
+        def words(columns):
+            return columns.rearrange("p (j t) -> p j t", t=PACK)
 
         def multiply_first(c):
             g, b = chunks[c]
@@ -215,15 +221,15 @@ def tile_list_forklift_tipping_features_kernel(
         def gate(c):
             at = 4 * KIB * c if c >= 2 else 4 * KIB + 2 * KIB * c
             gated[c] = staged.tile([P, PASS], F32, name="gated%d" % c, offset=at)
-            nc.scalar.activation(out=gated[c][:], in_=banks[c][0][:], func=ACT.Silu)
+            nc.scalar.activation(out=words(gated[c][:]), in_=across(banks[c][0]), func=ACT.Silu)
 
         def subtract(c):
             diff[c] = work.tile([P, PASS], F32, name="diff")
-            nc.vector.tensor_tensor(to_words(diff[c][:]), from_bank(gated[c]), from_bank(banks[c][1]), ALU.subtract)
+            nc.vector.tensor_tensor(words(diff[c][:]), words(gated[c][:]), across(banks[c][1]), ALU.subtract)
 
         def make_x(c):
             xz[c] = work.tile([P, 2 * PASS], BF16, name="xz", align_bytes=64, bufs=5)
-            nc.vector.tensor_tensor(to_words(xz[c][:, 0:PASS]), from_bank(banks[c][1]), factor(gl_sb, c), ALU.mult)
+            nc.vector.tensor_tensor(words(xz[c][:, 0:PASS]), across(banks[c][1]), factor(gl_sb, c), ALU.mult)
 
         def take_sine(c):
             at = 4 * KIB * (c + 2) + 2 * KIB if c < 6 else 2 * KIB * (c - 6)

@@ -26,6 +26,8 @@ BLOCKS = S // TRIPS
 GROUPS = H // PASS
 LIFT = S + H + N
 KIB = 1024
+EARLY = S + PASS
+PORT_ORDER = (0, 2, 1, 3)
 HALF = PASS // 2
 LINE = 16
 PIECES = 2
@@ -109,10 +111,10 @@ def tile_list_forklift_tipping_features_kernel(
             nc.vector.tensor_copy(picked[:], window.indirect(offsets[:]))
             return picked
 
-        def deal(dealt, size, packed):
+        def deal(dealt, size, packed, copy=nc.vector.tensor_copy):
             run = LINE // size
             groups = packed.shape[1]
-            nc.vector.tensor_copy(
+            copy(
                 out=dealt.rearrange("p (g t c u) -> p c g t u", g=groups, t=PACK, u=run),
                 in_=packed.rearrange("p g (c u t) -> p c g t u", t=PACK, u=run),
             )
@@ -140,13 +142,17 @@ def tile_list_forklift_tipping_features_kernel(
         nc.vector.tensor_copy(v_rows[:], tab_rows[:].indirect(idx[:]))
         deal(lift[:, S:LIFT], 1, by_group(w_rows))
         nc.vector.tensor_copy(lift[:, 0:S].bitcast(I32), v_rows[:].bitcast(I32))
-        for q in range(QUADRANTS):
-            nc.sync.dma_start(
-                out=planes[32 * q : 32 * q + ROWS, :].bitcast(I32).rearrange("r (a c) -> r a c", a=2),
-                in_=lift[96 + 2 * ROWS * q : 96 + 2 * ROWS * (q + 1), :].bitcast(I32))
+
+        def lift_rows(first, last):
+            for q in PORT_ORDER:
+                nc.sync.dma_start(
+                    out=planes[32 * q : 32 * q + ROWS, :].bitcast(I32).rearrange("r (a c) -> r a c", a=2)[:, :, first // 4 : last // 4],
+                    in_=lift[96 + 2 * ROWS * q : 96 + 2 * ROWS * (q + 1), first:last].bitcast(I32))
+
+        lift_rows(0, LIFT)
         load_words(tab2_w, tab2_words)
         v2_rows = gather("v2_rows", U8, tab2_rows[:], idx2)
-        for q in range(QUADRANTS):
+        for q in PORT_ORDER:
             nc.sync.dma_start(
                 out=v2_sc[32 * q : 32 * q + ROWS, :].bitcast(I32),
                 in_=v2_rows[112 + ROWS * q : 112 + ROWS * (q + 1), :].bitcast(I32))
@@ -154,23 +160,26 @@ def tile_list_forklift_tipping_features_kernel(
         load_factor(gs_sb, gs)
         v_w = [gather("v_w0", U32, tab_w[0][:], idx), held("v_w1", S, U32)]
         w1_w_dealt = [held("w1_w_dealt%d" % g, 2 * PASS, U16) for g in range(GROUPS)]
-        deal(w1_w_dealt[0][:], 2, by_group(w1_w[0]))
-        for h in range(2):
-            nc.vector.tensor_copy(
-                v_w[1][:, S // 2 * h : S // 2 * (h + 1)], tab_w[1][:].indirect(idx[:, S // 32 * h : S // 32 * (h + 1)]))
-        w2_q = [quantise("w2_0", w2_bf[0], PASS)]
+        deal(w1_w_dealt[0][:], 2, by_group(w1_w[0]), nc.scalar.copy)
         v2_w = held("v2_w", S, U16)
-        for h in range(2):
+
+        def gather_half(picked, window, offsets, h):
             nc.vector.tensor_copy(
-                v2_w[:, S // 2 * h : S // 2 * (h + 1)], tab2_w[:].indirect(idx2[:, S // 32 * h : S // 32 * (h + 1)]))
+                picked[:, S // 2 * h : S // 2 * (h + 1)], window[:].indirect(offsets[:, S // 32 * h : S // 32 * (h + 1)]))
+
+        gather_half(v_w[1], tab_w[1], idx, 0)
+        w2_q = [quantise("w2_0", w2_bf[0], PASS)]
+        gather_half(v2_w, tab2_w, idx2, 0)
+        gather_half(v_w[1], tab_w[1], idx, 1)
+        gather_half(v2_w, tab2_w, idx2, 1)
         load_rows(raw[2], w2[:, PASS : PASS + HALF])
         load_rows(raw[3], w2[:, PASS + HALF : 2 * PASS])
         load_words(w1_w[1], w1_words[:, :, 2 * PASS : 4 * PASS])
         load_rows(raw[4], w4[0:PASS, 0:HALF])
         load_rows(raw[5], w4[0:PASS, HALF:N])
-        load_words(w3_w, w3_words.rearrange("g p c i -> g p (c i)"))
         load_rows(raw[6], w4[PASS : 2 * PASS, 0:HALF])
         load_rows(raw[7], w4[PASS : 2 * PASS, HALF:N])
+        load_words(w3_w, w3_words.rearrange("g p c i -> g p (c i)"))
         w4_q = []
 
         chunks = [(g, b) for g in range(GROUPS) for b in range(BLOCKS)]
@@ -259,7 +268,7 @@ def tile_list_forklift_tipping_features_kernel(
         y_codes = held("y_codes", S, U32)
         y_plane = held("y_plane", S, U8)
 
-        def multiply_second(g, b):
+        def multiply_x(g, b, last=False):
             codes, plane = xz_q[g, b]
             for t in range(PACK):
                 nc.tensor.matmul_mx(
@@ -267,15 +276,18 @@ def tile_list_forklift_tipping_features_kernel(
                     lhsT=w3_w_dealt[:, N * g + P * t : N * g + P * (t + 1)].bitcast(FP8X4),
                     lhsT_scale=planes[:, LIFT * g + S + H + P * t : LIFT * g + S + H + P * (t + 1)],
                     rhs=codes[:, 0:TRIPS].bitcast(FP8X4), rhs_scale=plane[:, 0:TRIPS],
-                    start=(g == 0 and t == 0), stop=False,
+                    start=False, stop=False,
                 )
+
+        def multiply_z(g, b):
+            codes, plane = xz_q[g, b]
             w4_codes, w4_plane = w4_q[g]
             for t in range(PACK):
                 nc.tensor.matmul_mx(
                     out=y_banks[b][:, TRIPS * t : TRIPS * (t + 1)],
                     lhsT=w4_codes[:, P * t : P * (t + 1)].bitcast(FP8X4), lhsT_scale=w4_plane[:, P * t : P * (t + 1)],
                     rhs=codes[:, TRIPS : 2 * TRIPS].bitcast(FP8X4), rhs_scale=plane[:, TRIPS : 2 * TRIPS],
-                    start=False, stop=(g == GROUPS - 1 and t == PACK - 1),
+                    start=(g == 0 and t == 0), stop=(g == GROUPS - 1 and t == PACK - 1),
                 )
 
         y = [held("y%d" % b, PACK * TRIPS, F32) for b in range(BLOCKS)]
@@ -337,15 +349,20 @@ def tile_list_forklift_tipping_features_kernel(
                 quantised.append(quantise(name, rounded, PASS))
             if step == 2:
                 deal(w1_w_dealt[1][:], 2, by_group(w1_w[1]))
-            if step == 4:
+            if step == 5:
                 deal(w3_w_dealt[:], 4, by_group(w3_w))
             if 5 <= step < 7:
-                multiply_second(0, 2 * (step - 5))
-                multiply_second(0, 2 * (step - 5) + 1)
+                multiply_z(0, 2 * (step - 5))
+                multiply_z(0, 2 * (step - 5) + 1)
+            if step == 6:
+                for b in range(BLOCKS):
+                    multiply_x(0, b)
             if 7 <= step < count + 2:
-                multiply_second(1, step - 7)
+                multiply_x(1, step - 7)
+                multiply_z(1, step - 7)
                 store_y(step - 7)
-        multiply_second(1, 3)
+        multiply_x(1, 3)
+        multiply_z(1, 3)
         store_y(3)
 
         round_y(0)

@@ -26,6 +26,7 @@ BLOCKS = S // TRIPS
 GROUPS = H // PASS
 LIFT = S + H + N
 KIB = 1024
+VECTOR_Z = (0, 3, 7)
 EARLY = S + PASS
 PORT_ORDER = (0, 2, 1, 3)
 HALF = PASS // 2
@@ -247,7 +248,7 @@ def tile_list_forklift_tipping_features_kernel(
 
         def make_z(c):
             g = chunks[c][0]
-            engine = nc.gpsimd if c < count - 1 else nc.vector
+            engine = nc.vector if c in VECTOR_Z else nc.gpsimd
             engine.tensor_tensor(
                 xz[c][:, PASS : 2 * PASS].rearrange("p (j t) -> p j t", t=PACK),
                 sine[c][:].rearrange("p (j t) -> p j t", t=PACK),

@@ -64,15 +64,13 @@ def tile_list_forklift_tipping_features_kernel(
 
         tab_rows = held("tab_rows", T, U8)
         w_rows = held("w_rows", H + N, U8)
-        lift = held("lift", LIFT, U8)
-        planes = held("planes", 2 * LIFT, U8)
-        v2_sc = held("v2_sc", S, U8)
+        lift = held("lift", LIFT + S, U8)
+        planes = held("planes", 2 * LIFT + S, U8)
 
         nc.vector.memset(tab_rows[0:96, :].bitcast(I32), 0)
         nc.vector.memset(w_rows[0:96, :].bitcast(I32), 0)
-        nc.vector.memset(tab2_rows[0:112, :].bitcast(I32), 0)
+        nc.gpsimd.memset(tab2_rows[:].bitcast(I32), 0)
         nc.gpsimd.memset(planes[:].bitcast(I32), 0)
-        nc.vector.memset(v2_sc[:].bitcast(I32), 0)
 
         warm = held("warm", 16, F32)
         nc.gpsimd.memset(warm[:, 0:1], 0.0)
@@ -100,12 +98,11 @@ def tile_list_forklift_tipping_features_kernel(
         load_scale_rows(w_rows[96:P, 0:H], w1_scales)
         load_scale_rows(w_rows[96:P, H : H + N], w3_scales)
         nc.sync.dma_start(idx2[:], offs2)
-        load_scale_rows(tab2_rows[112:P, :], tab2_scales)
+        load_scale_rows(tab2_rows[97:P:2, :], tab2_scales)
         load_words(tab_w[0], tab_words[0:1].rearrange("g p c i -> g p (c i)"))
         load_rows(raw[0], w2[:, 0:HALF])
         load_words(w1_w[0], w1_words[:, :, 0 : 2 * PASS])
         load_words(tab_w[1], tab_words[1:2].rearrange("g p c i -> g p (c i)"))
-        load_rows(raw[1], w2[:, HALF:PASS])
 
         def gather(name, dtype, window, offsets):
             picked = held(name, S, dtype)
@@ -137,26 +134,25 @@ def tile_list_forklift_tipping_features_kernel(
 
         w2_bf = [held("w2_bf%d" % g, PACK * PASS, BF16) for g in range(GROUPS)]
         w4_bf = [held("w4_bf%d" % g, PACK * N, BF16) for g in range(GROUPS)]
-        for h in range(2):
-            round_and_deal(w2_bf[0], raw[h], slice(P // 2 * h, P // 2 * (h + 1)), slice(0, P // 2))
+        round_and_deal(w2_bf[0], raw[0], slice(0, P // 2), slice(0, P // 2))
 
         nc.vector.tensor_copy(v_rows[:], tab_rows[:].indirect(idx[:]))
         deal(lift[:, S:LIFT], 1, by_group(w_rows))
         nc.vector.tensor_copy(lift[:, 0:S].bitcast(I32), v_rows[:].bitcast(I32))
 
-        def lift_rows(first, last):
-            for q in PORT_ORDER:
+        def lift_rows(a, width):
+            for r in range(ROWS):
                 nc.sync.dma_start(
-                    out=planes[32 * q : 32 * q + ROWS, :].bitcast(I32).rearrange("r (a c) -> r a c", a=2)[:, :, first // 4 : last // 4],
-                    in_=lift[96 + 2 * ROWS * q : 96 + 2 * ROWS * (q + 1), first:last].bitcast(I32))
+                    out=planes[r:P:32, LIFT * a : LIFT * a + width].bitcast(I32),
+                    in_=lift[96 + 2 * r + a : P : 2 * ROWS, 0:width].bitcast(I32))
 
         lift_rows(0, LIFT)
-        load_words(tab2_w, tab2_words)
+        load_rows(raw[1], w2[:, HALF:PASS])
+        round_and_deal(w2_bf[0], raw[1], slice(P // 2, P), slice(0, P // 2))
         v2_rows = gather("v2_rows", U8, tab2_rows[:], idx2)
-        for q in PORT_ORDER:
-            nc.sync.dma_start(
-                out=v2_sc[32 * q : 32 * q + ROWS, :].bitcast(I32),
-                in_=v2_rows[112 + ROWS * q : 112 + ROWS * (q + 1), :].bitcast(I32))
+        nc.vector.tensor_copy(lift[:, LIFT : LIFT + S].bitcast(I32), v2_rows[:].bitcast(I32))
+        lift_rows(1, LIFT + S)
+        load_words(tab2_w, tab2_words)
         load_factor(gl_sb, gl)
         load_factor(gs_sb, gs)
         v_w = [gather("v_w0", U32, tab_w[0][:], idx), held("v_w1", S, U32)]
@@ -223,7 +219,7 @@ def tile_list_forklift_tipping_features_kernel(
                 nc.tensor.matmul_mx(
                     out=load_bank[:, TRIPS * t : TRIPS * (t + 1)],
                     lhsT=codes[:, P * t : P * (t + 1)].bitcast(FP8X4), lhsT_scale=plane[:, P * t : P * (t + 1)],
-                    rhs=v2_w[:, trips].bitcast(FP4X4), rhs_scale=v2_sc[:, trips],
+                    rhs=v2_w[:, trips].bitcast(FP4X4), rhs_scale=planes[:, 2 * LIFT + TRIPS * b : 2 * LIFT + TRIPS * (b + 1)],
                     start=True, stop=True,
                 )
             banks[c] = a_bank, load_bank

@@ -337,6 +337,11 @@ def tile_list_forklift_tipping_features_kernel(
                 for piece in range(PIECES // 2 * half, PIECES // 2 * (half + 1)):
                     width = P // PIECES
                     inside = piece - PIECES // 2 * half
+                    if step == 1:
+                        nc.gpsimd.tensor_scalar(
+                            w2_bf[1][:].rearrange("p (t m i) -> p m t i", t=PACK, i=PACK)[:, P // 2 : P],
+                            raw[3][:].rearrange("p (i m t) -> p m t i", i=PACK, t=PACK), 1.0, 0.0, ALU.mult, ALU.add)
+                        continue
                     round_and_deal(
                         late[weight][1], raw[2 + 2 * weight + half],
                         slice(width * piece, width * (piece + 1)), slice(width * inside, width * (inside + 1)),

@@ -24,15 +24,10 @@ ROWS = 4
 TRIPS = 128
 BLOCKS = S // TRIPS
 GROUPS = H // PASS
-LIFT = S + H + N
-KIB = 1024
-VECTOR_Z = (0, 3, 7)
-EARLY = S + PASS
-PORT_ORDER = (0, 2, 1, 3)
+LIFT = S + H
 HALF = PASS // 2
 LINE = 16
-PIECES = 2
-SCALAR_BLOCKS = 0
+GPSIMD_Z = (3, 4, 5, 6)
 
 
 def tile_list_forklift_tipping_features_kernel(
@@ -42,16 +37,14 @@ def tile_list_forklift_tipping_features_kernel(
     nc = tc.nc
     with ExitStack() as ctx:
         keep = ctx.enter_context(tc.tile_pool(name="keep", bufs=1))
-        work = ctx.enter_context(tc.tile_pool(name="work", bufs=3))
-        first_psum = ctx.enter_context(tc.psum_pool(name="first_psum", bufs=1))
-        second_psum = ctx.enter_context(tc.psum_pool(name="second_psum", bufs=1))
+        psum = ctx.enter_context(tc.psum_pool(name="psum", bufs=1))
 
-        def held(name, columns, dtype):
-            return keep.tile([P, columns], dtype, name=name, align_bytes=64)
+        def held(name, columns, dtype, tag=""):
+            return keep.tile([P, columns], dtype, name=name, align_bytes=64, tag=tag or name)
 
         idx = keep.tile([P, S // 16], U16, name="idx")
         idx2 = keep.tile([P, S // 16], U16, name="idx2")
-        tab_w = [held("tab_w%d" % k, T, U32) for k in range(2)]
+        tab_w = [held("tab_w0", T, U32), held("tab_w1", T, U32, "x_first")]
         tab2_w = held("tab2_w", T2, U16)
         w1_w = [held("w1_w%d" % g, 2 * PASS, U16) for g in range(GROUPS)]
         w3_w = held("w3_w", GROUPS * N, U32)
@@ -59,18 +52,19 @@ def tile_list_forklift_tipping_features_kernel(
         gs_sb = held("gs_sb", GROUPS * PACK, F32)
         v_rows = held("v_rows", S, U8)
         tab2_rows = held("tab2_rows", T2, U8)
-        staged = ctx.enter_context(tc.tile_pool(name="staged", bufs=1))
-        raw = [staged.tile([P, PACK * HALF], F32, name="raw%d" % h, offset=4 * KIB * h) for h in range(8)]
-
+        raw = [held("raw%d" % h, PACK * HALF, F32) for h in range(8)]
         tab_rows = held("tab_rows", T, U8)
-        w_rows = held("w_rows", H + N, U8)
-        lift = held("lift", LIFT + S, U8)
-        planes = held("planes", 2 * LIFT + S, U8)
+        w_rows = held("w_rows", H, U8)
+        w3_rows = held("w3_rows", N, U8)
+        w3_planes = held("w3_planes", N, U8)
+        lift = held("lift", LIFT, U8)
+        planes = held("planes", 2 * LIFT, U8)
 
         nc.vector.memset(tab_rows[0:96, :].bitcast(I32), 0)
         nc.vector.memset(w_rows[0:96, :].bitcast(I32), 0)
         nc.gpsimd.memset(tab2_rows[:].bitcast(I32), 0)
         nc.gpsimd.memset(planes[:].bitcast(I32), 0)
+        nc.gpsimd.memset(w3_rows[:].bitcast(I32), 0)
 
         warm = held("warm", 16, F32)
         nc.gpsimd.memset(warm[:, 0:1], 0.0)
@@ -93,21 +87,8 @@ def tile_list_forklift_tipping_features_kernel(
             nc.sync.dma_start(
                 out=tile[:].rearrange("p (g t) -> p g t", t=PACK), in_=factor.rearrange("(g p t) -> p g t", p=P, t=PACK))
 
-        nc.sync.dma_start(idx[:], offs)
-        load_scale_rows(tab_rows[96:P, :], tab_scales)
-        load_scale_rows(w_rows[96:P, 0:H], w1_scales)
-        load_scale_rows(w_rows[96:P, H : H + N], w3_scales)
-        nc.sync.dma_start(idx2[:], offs2)
-        load_scale_rows(tab2_rows[97:P:2, :], tab2_scales)
-        load_words(tab_w[0], tab_words[0:1].rearrange("g p c i -> g p (c i)"))
-        load_rows(raw[0], w2[:, 0:HALF])
-        load_words(w1_w[0], w1_words[:, :, 0 : 2 * PASS])
-        load_words(tab_w[1], tab_words[1:2].rearrange("g p c i -> g p (c i)"))
-
-        def gather(name, dtype, window, offsets):
-            picked = held(name, S, dtype)
-            nc.vector.tensor_copy(picked[:], window.indirect(offsets[:]))
-            return picked
+        def gather(picked, window, offsets):
+            nc.vector.tensor_copy(picked[:], window[:].indirect(offsets[:]))
 
         def deal(dealt, size, packed, copy=nc.vector.tensor_copy):
             run = LINE // size
@@ -120,73 +101,82 @@ def tile_list_forklift_tipping_features_kernel(
         def by_group(tile):
             return tile[:].rearrange("p (g c) -> p g c", c=PASS)
 
-        def round_and_deal(rounded, raw, part, raw_part, copy=nc.scalar.copy):
+        w_bf = [held("w_bf%d" % g, PACK * PASS, BF16) for g in range(4)]
+
+        def round_half(h, copy=nc.scalar.copy):
+            part = slice(P // 2 * (h % 2), P // 2 * (h % 2 + 1))
             copy(
-                out=rounded[:].rearrange("p (s e m i) -> p s m i e", s=2, e=2, i=PACK)[:, :, part],
-                in_=raw[:].rearrange("p (i m s e) -> p s m i e", i=PACK, s=2, e=2)[:, :, raw_part],
+                out=w_bf[h // 2][:].rearrange("p (s e m i) -> p s m i e", s=2, e=2, i=PACK)[:, :, part],
+                in_=raw[h][:].rearrange("p (i m s e) -> p s m i e", i=PACK, s=2, e=2),
             )
 
-        def quantise(name, values, columns):
-            codes = held(name + "_codes", columns, U32)
+        def quantise(name, values, columns, tag=""):
+            codes = held(name + "_codes", columns, U32, tag)
             plane = held(name + "_plane", columns, U8)
-            nc.vector.quantize_mx(out=codes[:].bitcast(FP8X4), scales=plane[:], in_=values[:])
+            nc.vector.quantize_mx(out=codes[:].bitcast(FP8X4), scales=plane[:], in_=values)
             return codes, plane
 
-        w2_bf = [held("w2_bf%d" % g, PACK * PASS, BF16) for g in range(GROUPS)]
-        w4_bf = [held("w4_bf%d" % g, PACK * N, BF16) for g in range(GROUPS)]
-        round_and_deal(w2_bf[0], raw[0], slice(0, P // 2), slice(0, P // 2))
-
-        nc.vector.tensor_copy(v_rows[:], tab_rows[:].indirect(idx[:]))
-        deal(lift[:, S:LIFT], 1, by_group(w_rows))
-        nc.vector.tensor_copy(lift[:, 0:S].bitcast(I32), v_rows[:].bitcast(I32))
-
-        def lift_rows(a, width):
+        def lift_rows(a):
             for r in range(ROWS):
                 nc.sync.dma_start(
-                    out=planes[r:P:32, LIFT * a : LIFT * a + width].bitcast(I32),
-                    in_=lift[96 + 2 * r + a : P : 2 * ROWS, 0:width].bitcast(I32))
+                    out=planes[r:P:32, LIFT * a : LIFT * (a + 1)].bitcast(I32),
+                    in_=lift[96 + 2 * r + a : P : 2 * ROWS, :].bitcast(I32))
 
-        lift_rows(0, LIFT)
-        load_rows(raw[1], w2[:, HALF:PASS])
-        round_and_deal(w2_bf[0], raw[1], slice(P // 2, P), slice(0, P // 2))
-        v2_rows = gather("v2_rows", U8, tab2_rows[:], idx2)
-        nc.vector.tensor_copy(lift[:, LIFT : LIFT + S].bitcast(I32), v2_rows[:].bitcast(I32))
-        lift_rows(1, LIFT + S)
+        nc.sync.dma_start(idx[:], offs)
+        load_scale_rows(tab_rows[96:P, :], tab_scales)
+        nc.sync.dma_start(idx2[:], offs2)
         load_words(tab2_w, tab2_words)
+        load_rows(raw[0], w2[:, 0:HALF])
+        for r in range(ROWS):
+            nc.sync.dma_start(
+                out=tab2_rows[r:P:32, :].bitcast(I32),
+                in_=tab2_scales[0].rearrange("(q r) c -> r q c", r=ROWS)[r].bitcast(I32))
+        load_rows(raw[1], w2[:, HALF:PASS])
+        load_scale_rows(w_rows[96:P, :], w1_scales)
+        load_words(tab_w[0], tab_words[0:1].rearrange("g p c i -> g p (c i)"))
         load_factor(gl_sb, gl)
-        load_factor(gs_sb, gs)
-        v_w = [gather("v_w0", U32, tab_w[0][:], idx), held("v_w1", S, U32)]
-        w1_w_dealt = [held("w1_w_dealt%d" % g, 2 * PASS, U16) for g in range(GROUPS)]
-        deal(w1_w_dealt[0][:], 2, by_group(w1_w[0]), nc.scalar.copy)
+        load_words(tab_w[1], tab_words[1:2].rearrange("g p c i -> g p (c i)"))
+        load_words(w1_w[0], w1_words[:, :, 0 : 2 * PASS])
+
         v2_w = held("v2_w", S, U16)
+        v2_plane = held("v2_plane", S, U8)
+        w1_w_dealt = [held("w1_w_dealt%d" % g, 2 * PASS, U16) for g in range(GROUPS)]
+        w3_w_dealt = held("w3_w_dealt", GROUPS * N, U32)
 
-        def gather_half(picked, window, offsets, h):
-            nc.vector.tensor_copy(
-                picked[:, S // 2 * h : S // 2 * (h + 1)], window[:].indirect(offsets[:, S // 32 * h : S // 32 * (h + 1)]))
+        gather(v_rows, tab_rows, idx)
+        gather(v2_w, tab2_w, idx2)
+        gather(v2_plane, tab2_rows, idx2)
+        deal(lift[:, S:LIFT], 1, by_group(w_rows))
+        nc.vector.tensor_copy(lift[:, 0:S].bitcast(I32), v_rows[:].bitcast(I32))
+        round_half(0)
+        round_half(1)
 
-        gather_half(v_w[1], tab_w[1], idx, 0)
-        w2_q = [quantise("w2_0", w2_bf[0], PASS)]
-        gather_half(v2_w, tab2_w, idx2, 0)
-        gather_half(v_w[1], tab_w[1], idx, 1)
-        gather_half(v2_w, tab2_w, idx2, 1)
+        lift_rows(0)
         load_rows(raw[2], w2[:, PASS : PASS + HALF])
-        load_rows(raw[3], w2[:, PASS + HALF : 2 * PASS])
+        lift_rows(1)
         load_words(w1_w[1], w1_words[:, :, 2 * PASS : 4 * PASS])
+        load_rows(raw[3], w2[:, PASS + HALF : 2 * PASS])
+        load_factor(gs_sb, gs)
         load_rows(raw[4], w4[0:PASS, 0:HALF])
         load_rows(raw[5], w4[0:PASS, HALF:N])
+        load_words(w3_w, w3_words.rearrange("g p c i -> g p (c i)"))
         load_rows(raw[6], w4[PASS : 2 * PASS, 0:HALF])
         load_rows(raw[7], w4[PASS : 2 * PASS, HALF:N])
-        load_words(w3_w, w3_words.rearrange("g p c i -> g p (c i)"))
-        w4_q = []
+        for q in range(QUADRANTS):
+            nc.sync.dma_start(
+                out=w3_rows[32 * q + ROWS : 32 * q + 3 * ROWS, :].bitcast(I32),
+                in_=w3_scales[:, ROWS * q : ROWS * (q + 1), :].bitcast(I32))
+
+        w_q = [quantise("w_q0", w_bf[0][:], PASS)]
+        v_w = [held("v_w%d" % k, S, U32) for k in range(2)]
+        gather(v_w[0], tab_w[0], idx)
+        gather(v_w[1], tab_w[1], idx)
+        deal(w1_w_dealt[0][:], 2, by_group(w1_w[0]), nc.scalar.copy)
+        round_half(2)
 
         chunks = [(g, b) for g in range(GROUPS) for b in range(BLOCKS)]
-        banks, gated, diff, sine, xz, xz_q = {}, {}, {}, {}, {}, {}
-
-        def from_bank(bank):
-            return bank[:].rearrange("p (t c e) -> p c t e", t=PACK, e=2)
-
-        def to_words(columns):
-            return columns.rearrange("p (c e t) -> p c t e", t=PACK, e=2)
+        a_banks, load_banks, y_banks, gated, diff, sine = {}, {}, {}, {}, {}, {}
+        x_at, z_at, x_q, z_q = {}, {}, {}, {}
 
         def factor(tile, c):
             g = chunks[c][0]
@@ -198,97 +188,85 @@ def tile_list_forklift_tipping_features_kernel(
         def words(columns):
             return columns.rearrange("p (j t) -> p j t", t=PACK)
 
-        def multiply_first(c):
+        def multiply_a(c):
             g, b = chunks[c]
             trips = slice(TRIPS * b, TRIPS * (b + 1))
-            swap = 0 if c < 2 else 1
-            a_bank = first_psum.tile([P, PASS], F32, name="a_bank", tag="bank%d" % (2 * (c % 2) + swap))
-            load_bank = first_psum.tile([P, PASS], F32, name="load_bank", tag="bank%d" % (2 * (c % 2) + 1 - swap))
-            for t in range(PACK):
-                for k in range(2):
+            a_banks[c] = psum.tile([P, PASS], F32, name="a_bank%d" % c, tag="bank%d" % (BLOCKS + b))
+            for k in range(2):
+                for t in range(PACK):
                     first = LIFT * k + S + PASS * g + P * t
                     nc.tensor.matmul_mx(
-                        out=a_bank[:, TRIPS * t : TRIPS * (t + 1)],
+                        out=a_banks[c][:, TRIPS * t : TRIPS * (t + 1)],
                         lhsT=w1_w_dealt[g][:, PASS * k + P * t : PASS * k + P * (t + 1)].bitcast(FP4X4),
                         lhsT_scale=planes[:, first : first + P],
-                        rhs=v_w[k][:, trips].bitcast(FP8X4), rhs_scale=planes[:, LIFT * k + TRIPS * b : LIFT * k + TRIPS * (b + 1)],
-                        start=(k == 0), stop=(k == 1),
+                        rhs=v_w[k][:, trips].bitcast(FP8X4),
+                        rhs_scale=planes[:, LIFT * k + TRIPS * b : LIFT * k + TRIPS * (b + 1)],
+                        start=(k == 0 and t == 0), stop=(k == 1 and t == PACK - 1),
                     )
-            codes, plane = w2_q[g]
+
+        def multiply_load(c):
+            g, b = chunks[c]
+            trips = slice(TRIPS * b, TRIPS * (b + 1))
+            load_banks[c] = psum.tile([P, PASS], F32, name="load_bank%d" % c, tag="bank%d" % b)
+            codes, plane = w_q[g]
             for t in range(PACK):
                 nc.tensor.matmul_mx(
-                    out=load_bank[:, TRIPS * t : TRIPS * (t + 1)],
+                    out=load_banks[c][:, TRIPS * t : TRIPS * (t + 1)],
                     lhsT=codes[:, P * t : P * (t + 1)].bitcast(FP8X4), lhsT_scale=plane[:, P * t : P * (t + 1)],
-                    rhs=v2_w[:, trips].bitcast(FP4X4), rhs_scale=planes[:, 2 * LIFT + TRIPS * b : 2 * LIFT + TRIPS * (b + 1)],
+                    rhs=v2_w[:, trips].bitcast(FP4X4), rhs_scale=v2_plane[:, trips],
                     start=True, stop=True,
                 )
-            banks[c] = a_bank, load_bank
 
         def gate(c):
-            at = 4 * KIB * c if c >= 2 else 4 * KIB + 2 * KIB * c
-            gated[c] = staged.tile([P, PASS], F32, name="gated%d" % c, offset=at)
-            nc.scalar.activation(out=words(gated[c][:]), in_=across(banks[c][0]), func=ACT.Silu)
+            gated[c] = held("gated%d" % c, PASS, F32)
+            nc.scalar.activation(out=words(gated[c][:]), in_=across(a_banks[c]), func=ACT.Silu)
 
         def subtract(c):
-            diff[c] = work.tile([P, PASS], F32, name="diff")
-            nc.vector.tensor_tensor(words(diff[c][:]), words(gated[c][:]), across(banks[c][1]), ALU.subtract)
-
-        def make_x(c):
-            xz[c] = work.tile([P, 2 * PASS], BF16, name="xz", align_bytes=64, bufs=5)
-            nc.vector.tensor_tensor(words(xz[c][:, 0:PASS]), across(banks[c][1]), factor(gl_sb, c), ALU.mult)
+            diff[c] = held("diff%d" % c, PASS, F32)
+            nc.vector.tensor_tensor(words(diff[c][:]), words(gated[c][:]), across(load_banks[c]), ALU.subtract)
 
         def take_sine(c):
-            at = 4 * KIB * (c + 2) + 2 * KIB if c < 6 else 2 * KIB * (c - 6)
-            sine[c] = staged.tile([P, PASS], F32, name="sine%d" % c, offset=at)
+            sine[c] = held("sine%d" % c, PASS, F32)
             nc.scalar.activation(out=sine[c][:], in_=diff[c][:], func=ACT.Sin)
 
+        def make_x(c):
+            nc.vector.tensor_tensor(words(x_at[c]), across(load_banks[c]), factor(gl_sb, c), ALU.mult)
+
         def make_z(c):
-            g = chunks[c][0]
-            engine = nc.vector if c in VECTOR_Z else nc.gpsimd
-            engine.tensor_tensor(
-                xz[c][:, PASS : 2 * PASS].rearrange("p (j t) -> p j t", t=PACK),
-                sine[c][:].rearrange("p (j t) -> p j t", t=PACK),
-                gs_sb[:, PACK * g : PACK * (g + 1)].unsqueeze(1).to_broadcast([P, TRIPS, PACK]), ALU.mult)
+            engine = nc.gpsimd if c in GPSIMD_Z else nc.vector
+            engine.tensor_tensor(words(z_at[c]), words(sine[c][:]), factor(gs_sb, c), ALU.mult)
 
-        def quantise_chunk(c):
-            xz_q[chunks[c]] = quantise("xz%d" % c, xz[c], 2 * TRIPS)
+        def operand(pair, j):
+            codes, plane = pair
+            return codes[:, TRIPS * j : TRIPS * (j + 1)].bitcast(FP8X4), plane[:, TRIPS * j : TRIPS * (j + 1)]
 
-        def quantise_half(c, half):
-            if half == 0:
-                xz_q[chunks[c]] = held("last_codes", 2 * TRIPS, U32), held("last_plane", 2 * TRIPS, U8)
-            codes, plane = xz_q[chunks[c]]
-            words = slice(TRIPS * half, TRIPS * (half + 1))
-            nc.vector.quantize_mx(
-                out=codes[:, words].bitcast(FP8X4), scales=plane[:, words], in_=xz[c][:, PASS * half : PASS * (half + 1)])
-
-        y_banks = [second_psum.tile([P, PASS], F32, name="y_bank%d" % b) for b in range(BLOCKS)]
-        y_codes = held("y_codes", S, U32)
-        y_plane = held("y_plane", S, U8)
-
-        def multiply_x(g, b, last=False):
-            codes, plane = xz_q[g, b]
+        def multiply_x(g, b):
+            codes, plane = x_q[BLOCKS * g + b]
             for t in range(PACK):
                 nc.tensor.matmul_mx(
                     out=y_banks[b][:, TRIPS * t : TRIPS * (t + 1)],
                     lhsT=w3_w_dealt[:, N * g + P * t : N * g + P * (t + 1)].bitcast(FP8X4),
-                    lhsT_scale=planes[:, LIFT * g + S + H + P * t : LIFT * g + S + H + P * (t + 1)],
-                    rhs=codes[:, 0:TRIPS].bitcast(FP8X4), rhs_scale=plane[:, 0:TRIPS],
-                    start=False, stop=False,
+                    lhsT_scale=w3_planes[ROWS * (g + 1) : P, P * t : P * (t + 1)],
+                    rhs=codes, rhs_scale=plane, start=False, stop=False,
                 )
 
         def multiply_z(g, b):
-            codes, plane = xz_q[g, b]
-            w4_codes, w4_plane = w4_q[g]
+            if g == 0:
+                y_banks[b] = psum.tile([P, PASS], F32, name="y_bank%d" % b, tag="bank%d" % (BLOCKS, BLOCKS + 1, 0, 1)[b])
+            codes, plane = z_q[BLOCKS * g + b]
+            w4_codes, w4_plane = w_q[2 + g]
             for t in range(PACK):
                 nc.tensor.matmul_mx(
                     out=y_banks[b][:, TRIPS * t : TRIPS * (t + 1)],
                     lhsT=w4_codes[:, P * t : P * (t + 1)].bitcast(FP8X4), lhsT_scale=w4_plane[:, P * t : P * (t + 1)],
-                    rhs=codes[:, TRIPS : 2 * TRIPS].bitcast(FP8X4), rhs_scale=plane[:, TRIPS : 2 * TRIPS],
+                    rhs=codes, rhs_scale=plane,
                     start=(g == 0 and t == 0), stop=(g == GROUPS - 1 and t == PACK - 1),
                 )
 
         y = [held("y%d" % b, PACK * TRIPS, F32) for b in range(BLOCKS)]
         y_bf = held("y_bf", PACK * S, BF16)
+        y_codes = held("y_codes", S, U32)
+        y_plane = held("y_plane", S, U8)
 
         def store_y(b):
             nc.scalar.copy(out=y[b][:], in_=y_banks[b][:])
@@ -298,11 +276,9 @@ def tile_list_forklift_tipping_features_kernel(
             )
 
         def round_y(b):
-            rounded = to_words(y_bf[:, PASS * b : PASS * (b + 1)])
-            if b < SCALAR_BLOCKS:
-                nc.scalar.copy(out=rounded, in_=from_bank(y_banks[b]))
-            else:
-                nc.vector.tensor_copy(out=rounded, in_=from_bank(y[b]))
+            nc.vector.tensor_copy(
+                out=y_bf[:, PASS * b : PASS * (b + 1)].rearrange("p (c e t) -> p c t e", t=PACK, e=2),
+                in_=y[b][:].rearrange("p (t c e) -> p c t e", t=PACK, e=2))
 
         def quantise_y(first, last):
             trips = slice(TRIPS * first, TRIPS * last)
@@ -314,58 +290,78 @@ def tile_list_forklift_tipping_features_kernel(
             nc.sync.dma_start(
                 out=out_1[0].rearrange("p m t -> p (m t)").bitcast(I32)[:, trips], in_=y_codes[:, trips].bitcast(I32))
 
-        late = [("w2_1", w2_bf[1], w2_q), ("w4_0", w4_bf[0], w4_q), ("w4_1", w4_bf[1], w4_q)]
+        x_first = held("x_first_bf", BLOCKS * PASS, BF16, "x_first")
+        z_first = [held("z_first%d" % j, 2 * PASS, BF16) for j in range(2)]
+        xz = [held("xz%d" % b, 2 * PASS, BF16) for b in range(BLOCKS)]
+        for b in range(BLOCKS):
+            x_at[b] = x_first[:, PASS * b : PASS * (b + 1)]
+            z_at[b] = z_first[b // 2][:, PASS * (b % 2) : PASS * (b % 2 + 1)]
+            x_at[BLOCKS + b] = xz[b][:, 0:PASS]
+            z_at[BLOCKS + b] = xz[b][:, PASS : 2 * PASS]
+        for c in range(BLOCKS):
+            multiply_load(c)
+        for c in range(BLOCKS):
+            make_x(c)
+        for c in range(BLOCKS):
+            multiply_a(c)
+
         count = len(chunks)
-        w3_w_dealt = held("w3_w_dealt", GROUPS * N, U32)
+        last = count - 1
+        gate(0)
+        gate(1)
+        nc.gpsimd.tensor_scalar(
+            w_bf[1][:].rearrange("p (t m i) -> p m t i", t=PACK, i=PACK)[:, P // 2 : P],
+            raw[3][:].rearrange("p (i m t) -> p m t i", i=PACK, t=PACK), 1.0, 0.0, ALU.mult, ALU.add)
         for step in range(count + 2):
             if step < count:
-                multiply_first(step)
-                gate(step)
-            if 1 <= step <= count:
-                subtract(step - 1)
-                take_sine(step - 1)
-            if 2 <= step < count + 2:
-                make_z(step - 2)
-            if 1 <= step <= count:
-                make_x(step - 1)
-            if 3 <= step < count + 2:
-                quantise_chunk(step - 3)
-            if count <= step < count + 2:
-                quantise_half(count - 1, step - count)
-            weight, half = divmod(step, 2)
-            if 0 <= weight < len(late):
-                for piece in range(PIECES // 2 * half, PIECES // 2 * (half + 1)):
-                    width = P // PIECES
-                    inside = piece - PIECES // 2 * half
-                    if step == 1:
-                        nc.gpsimd.tensor_scalar(
-                            w2_bf[1][:].rearrange("p (t m i) -> p m t i", t=PACK, i=PACK)[:, P // 2 : P],
-                            raw[3][:].rearrange("p (i m t) -> p m t i", i=PACK, t=PACK), 1.0, 0.0, ALU.mult, ALU.add)
-                        continue
-                    round_and_deal(
-                        late[weight][1], raw[2 + 2 * weight + half],
-                        slice(width * piece, width * (piece + 1)), slice(width * inside, width * (inside + 1)),
-                        nc.vector.tensor_copy if step == 3 else nc.scalar.copy)
-            if half == 0 and 1 <= weight <= len(late):
-                name, rounded, quantised = late[weight - 1]
-                quantised.append(quantise(name, rounded, PASS))
-            if step == 2:
+                subtract(step)
+                take_sine(step)
+            if BLOCKS <= step < count:
+                make_x(step)
+            if step == 0:
                 deal(w1_w_dealt[1][:], 2, by_group(w1_w[1]))
-            if step == 5:
+            if BLOCKS <= step + 2 < count:
+                multiply_a(step + 2)
+            if step + 2 < count:
+                gate(step + 2)
+            if step == count:
+                x_q[last] = operand(quantise("x_last", x_at[last], TRIPS), 0)
+            if 1 <= step <= count:
+                make_z(step - 1)
+            if step == 1:
+                pair = quantise("x_first", x_first[:], S, "gated1")
+                for b in range(BLOCKS):
+                    x_q[b] = operand(pair, b)
+                w_q.append(quantise("w_q1", w_bf[1][:], PASS))
+            if BLOCKS <= step + 2 < count:
+                multiply_load(step + 2)
+            if step == 4:
                 deal(w3_w_dealt[:], 4, by_group(w3_w))
-            if 5 <= step < 7:
-                multiply_z(0, 2 * (step - 5))
-                multiply_z(0, 2 * (step - 5) + 1)
+            if step == 6:
+                deal(w3_planes[:], 1, by_group(w3_rows))
+            if 2 <= step < 6:
+                round_half(step + 2)
+            if step in (4, 6):
+                w_q.append(quantise("w_q%d" % (step // 2), w_bf[step // 2][:], PASS))
+            if step in (3, 5):
+                j = step // 2 - 1
+                pair = quantise("z_first%d" % j, z_first[j][:], 2 * TRIPS)
+                z_q[2 * j], z_q[2 * j + 1] = operand(pair, 0), operand(pair, 1)
+            if step in (4, 5):
+                for b in (2 * (step - 4), 2 * (step - 4) + 1):
+                    multiply_z(0, b)
             if step == 6:
                 for b in range(BLOCKS):
                     multiply_x(0, b)
-            if 7 <= step < count + 2:
-                multiply_x(1, step - 7)
-                multiply_z(1, step - 7)
-                store_y(step - 7)
-        multiply_x(1, 3)
-        multiply_z(1, 3)
-        store_y(3)
+            if BLOCKS <= step - 2 < last:
+                pair = quantise("xz%d" % step, xz[step - 2 - BLOCKS][:], 2 * TRIPS)
+                x_q[step - 2], z_q[step - 2] = operand(pair, 0), operand(pair, 1)
+            if step == count + 1:
+                z_q[last] = operand(quantise("z_last", z_at[last], TRIPS), 0)
+            if step >= 6:
+                multiply_x(1, step - 6)
+                multiply_z(1, step - 6)
+                store_y(step - 6)
 
         round_y(0)
         round_y(1)

@@ -340,7 +340,7 @@ def tile_list_forklift_tipping_features_kernel(
             if step == 6:
                 deal(w3_planes[:], 1, by_group(w3_rows))
             if 2 <= step < 6:
-                round_half(step + 2)
+                round_half(step + 2, nc.vector.tensor_copy if step < 4 else nc.scalar.copy)
             if step in (4, 6):
                 w_q.append(quantise("w_q%d" % (step // 2), w_bf[step // 2][:], PASS))
             if step in (3, 5):

@@ -62,7 +62,9 @@ def tile_list_forklift_tipping_features_kernel(
 
         nc.vector.memset(tab_rows[0:96, :].bitcast(I32), 0)
         nc.vector.memset(w_rows[0:96, :].bitcast(I32), 0)
-        nc.gpsimd.memset(tab2_rows[:].bitcast(I32), 0)
+        nc.gpsimd.memset(tab2_rows[0:112, :].bitcast(I32), 0)
+        v2_plane = held("v2_plane", S, U8)
+        nc.gpsimd.memset(v2_plane[:].bitcast(I32), 0)
         nc.gpsimd.memset(planes[:].bitcast(I32), 0)
         nc.gpsimd.memset(w3_rows[:].bitcast(I32), 0)
 
@@ -122,30 +124,30 @@ def tile_list_forklift_tipping_features_kernel(
                     out=planes[r:P:32, LIFT * a : LIFT * (a + 1)].bitcast(I32),
                     in_=lift[96 + 2 * r + a : P : 2 * ROWS, :].bitcast(I32))
 
+        nc.sync.dma_start(idx2[:], offs2)
+        load_scale_rows(tab2_rows[112:P, :], tab2_scales)
         nc.sync.dma_start(idx[:], offs)
         load_scale_rows(tab_rows[96:P, :], tab_scales)
-        nc.sync.dma_start(idx2[:], offs2)
         load_words(tab2_w, tab2_words)
         load_rows(raw[0], w2[:, 0:HALF])
-        for r in range(ROWS):
-            nc.sync.dma_start(
-                out=tab2_rows[r:P:32, :].bitcast(I32),
-                in_=tab2_scales[0].rearrange("(q r) c -> r q c", r=ROWS)[r].bitcast(I32))
         load_rows(raw[1], w2[:, HALF:PASS])
         load_scale_rows(w_rows[96:P, :], w1_scales)
+
+        v2_w = held("v2_w", S, U16)
+        w1_w_dealt = [held("w1_w_dealt%d" % g, 2 * PASS, U16) for g in range(GROUPS)]
+        w3_w_dealt = held("w3_w_dealt", GROUPS * N, U32)
+
+        v2_rows = held("v2_rows", S, U8)
+        gather(v2_rows, tab2_rows, idx2)
+        for r in range(ROWS):
+            nc.sync.dma_start(
+                out=v2_plane[r:P:32, :].bitcast(I32), in_=v2_rows[112 + r : P : ROWS, :].bitcast(I32))
         load_words(tab_w[0], tab_words[0:1].rearrange("g p c i -> g p (c i)"))
         load_factor(gl_sb, gl)
         load_words(tab_w[1], tab_words[1:2].rearrange("g p c i -> g p (c i)"))
         load_words(w1_w[0], w1_words[:, :, 0 : 2 * PASS])
-
-        v2_w = held("v2_w", S, U16)
-        v2_plane = held("v2_plane", S, U8)
-        w1_w_dealt = [held("w1_w_dealt%d" % g, 2 * PASS, U16) for g in range(GROUPS)]
-        w3_w_dealt = held("w3_w_dealt", GROUPS * N, U32)
-
         gather(v_rows, tab_rows, idx)
         gather(v2_w, tab2_w, idx2)
-        gather(v2_plane, tab2_rows, idx2)
         deal(lift[:, S:LIFT], 1, by_group(w_rows))
         nc.vector.tensor_copy(lift[:, 0:S].bitcast(I32), v_rows[:].bitcast(I32))
         round_half(0)
@@ -374,7 +376,7 @@ def tile_list_forklift_tipping_features_kernel(
         store_codes(3, 4)
 
         for q in range(QUADRANTS):
-            nc.scalar.dma_start(
+            (nc.scalar if q < 3 else nc.sync).dma_start(
                 out=out_2[0, ROWS * q : ROWS * (q + 1), :].bitcast(I32),
                 in_=y_plane[32 * q : 32 * q + ROWS, :].bitcast(I32),
             )

from contextlib import ExitStack

import concourse.mybir as mybir

K, K2, T, T2, S, H, N = 1024, 512, 1024, 2048, 512, 1024, 512
FLOPS = 2 * S * H * (K + K2 + 2 * N)

F32 = mybir.dt.float32
BF16 = mybir.dt.bfloat16
I32 = mybir.dt.int32
U32 = mybir.dt.uint32
U16 = mybir.dt.uint16
U8 = mybir.dt.uint8
FP8X4 = mybir.dt.float8_e4m3fn_x4
FP4X4 = mybir.dt.float4_e2m1fn_x4
ACT = mybir.ActivationFunctionType
ALU = mybir.AluOpType

P = 128
PACK = 4
PASS = P * PACK
QUADRANTS = 4
ROWS = 4
TRIPS = 128
BLOCKS = S // TRIPS
GROUPS = H // PASS
LIFT = S + H
HALF = PASS // 2
LINE = 16
GPSIMD_Z = (3, 4, 5, 6)


def tile_list_forklift_tipping_features_kernel(
    tc, tab_words, tab_scales, tab2_words, tab2_scales, offs, offs2,
    w1_words, w1_scales, w2, w3_words, w3_scales, w4, gl, gs, out_0, out_1, out_2,
):
    nc = tc.nc
    with ExitStack() as ctx:
        keep = ctx.enter_context(tc.tile_pool(name="keep", bufs=1))
        psum = ctx.enter_context(tc.psum_pool(name="psum", bufs=1))

        def held(name, columns, dtype, tag=""):
            return keep.tile([P, columns], dtype, name=name, align_bytes=64, tag=tag or name)

        idx = keep.tile([P, S // 16], U16, name="idx")
        idx2 = keep.tile([P, S // 16], U16, name="idx2")
        tab_w = [held("tab_w0", T, U32), held("tab_w1", T, U32, "x_first")]
        tab2_w = held("tab2_w", T2, U16)
        w1_w = [held("w1_w%d" % g, 2 * PASS, U16) for g in range(GROUPS)]
        w3_w = held("w3_w", GROUPS * N, U32)
        gl_sb = held("gl_sb", GROUPS * PACK, F32)
        gs_sb = held("gs_sb", GROUPS * PACK, F32)
        v_rows = held("v_rows", S, U8)
        tab2_rows = held("tab2_rows", T2, U8)
        raw = [held("raw%d" % h, PACK * HALF, F32) for h in range(8)]
        tab_rows = held("tab_rows", T, U8)
        w_rows = held("w_rows", H, U8)
        w3_rows = held("w3_rows", N, U8)
        w3_planes = held("w3_planes", N, U8)
        lift = held("lift", LIFT, U8)
        planes = held("planes", 2 * LIFT, U8)

        nc.vector.memset(tab_rows[0:96, :].bitcast(I32), 0)
        nc.vector.memset(w_rows[0:96, :].bitcast(I32), 0)
        nc.gpsimd.memset(tab2_rows[0:112, :].bitcast(I32), 0)
        v2_plane = held("v2_plane", S, U8)
        nc.gpsimd.memset(v2_plane[:].bitcast(I32), 0)
        nc.gpsimd.memset(planes[:].bitcast(I32), 0)
        nc.gpsimd.memset(w3_rows[:].bitcast(I32), 0)

        warm = held("warm", 16, F32)
        nc.gpsimd.memset(warm[:, 0:1], 0.0)
        nc.scalar.activation(out=warm[:, 8:9], in_=warm[:, 0:1], func=ACT.Silu)

        def load_words(tile, words):
            nc.sync.dma_start(
                out=tile[:].bitcast(I32).rearrange("p (g c) -> p g c", g=words.shape[0]),
                in_=words.bitcast(I32).rearrange("g p c -> p g c"),
            )

        def load_scale_rows(rows, scales):
            nc.sync.dma_start(out=rows.bitcast(I32), in_=scales.bitcast(I32).rearrange("a q c -> q a c"))

        def load_rows(tile, rows):
            nc.sync.dma_start(
                out=tile[:].rearrange("p (i c) -> p i c", i=PACK), in_=rows.rearrange("(p i) c -> p i c", i=PACK))

        def load_factor(tile, factor):
            nc.sync.dma_start(
                out=tile[:].rearrange("p (g t) -> p g t", t=PACK), in_=factor.rearrange("(g p t) -> p g t", p=P, t=PACK))

        def gather(picked, window, offsets):
            nc.vector.tensor_copy(picked[:], window[:].indirect(offsets[:]))

        def deal(dealt, size, packed, copy=nc.vector.tensor_copy):
            run = LINE // size
            groups = packed.shape[1]
            copy(
                out=dealt.rearrange("p (g t c u) -> p c g t u", g=groups, t=PACK, u=run),
                in_=packed.rearrange("p g (c u t) -> p c g t u", t=PACK, u=run),
            )

        def by_group(tile):
            return tile[:].rearrange("p (g c) -> p g c", c=PASS)

        w_bf = [held("w_bf%d" % g, PACK * PASS, BF16) for g in range(4)]

        def round_half(h, copy=nc.scalar.copy):
            part = slice(P // 2 * (h % 2), P // 2 * (h % 2 + 1))
            copy(
                out=w_bf[h // 2][:].rearrange("p (s e m i) -> p s m i e", s=2, e=2, i=PACK)[:, :, part],
                in_=raw[h][:].rearrange("p (i m s e) -> p s m i e", i=PACK, s=2, e=2),
            )

        def quantise(name, values, columns, tag=""):
            codes = held(name + "_codes", columns, U32, tag)
            plane = held(name + "_plane", columns, U8)
            nc.vector.quantize_mx(out=codes[:].bitcast(FP8X4), scales=plane[:], in_=values)
            return codes, plane

        def lift_rows(a):
            for r in range(ROWS):
                nc.sync.dma_start(
                    out=planes[r:P:32, LIFT * a : LIFT * (a + 1)].bitcast(I32),
                    in_=lift[96 + 2 * r + a : P : 2 * ROWS, :].bitcast(I32))

        nc.sync.dma_start(idx2[:], offs2)
        load_scale_rows(tab2_rows[112:P, :], tab2_scales)
        nc.sync.dma_start(idx[:], offs)
        load_scale_rows(tab_rows[96:P, :], tab_scales)
        load_words(tab2_w, tab2_words)
        load_rows(raw[0], w2[:, 0:HALF])
        load_rows(raw[1], w2[:, HALF:PASS])
        load_scale_rows(w_rows[96:P, :], w1_scales)

        v2_w = held("v2_w", S, U16)
        w1_w_dealt = [held("w1_w_dealt%d" % g, 2 * PASS, U16) for g in range(GROUPS)]
        w3_w_dealt = held("w3_w_dealt", GROUPS * N, U32)

        v2_rows = held("v2_rows", S, U8)
        gather(v2_rows, tab2_rows, idx2)
        for r in range(ROWS):
            nc.sync.dma_start(
                out=v2_plane[r:P:32, :].bitcast(I32), in_=v2_rows[112 + r : P : ROWS, :].bitcast(I32))
        load_words(tab_w[0], tab_words[0:1].rearrange("g p c i -> g p (c i)"))
        load_factor(gl_sb, gl)
        load_words(tab_w[1], tab_words[1:2].rearrange("g p c i -> g p (c i)"))
        load_words(w1_w[0], w1_words[:, :, 0 : 2 * PASS])
        gather(v_rows, tab_rows, idx)
        gather(v2_w, tab2_w, idx2)
        deal(lift[:, S:LIFT], 1, by_group(w_rows))
        nc.vector.tensor_copy(lift[:, 0:S].bitcast(I32), v_rows[:].bitcast(I32))
        round_half(0)
        round_half(1)

        lift_rows(0)
        load_rows(raw[2], w2[:, PASS : PASS + HALF])
        lift_rows(1)
        load_words(w1_w[1], w1_words[:, :, 2 * PASS : 4 * PASS])
        load_rows(raw[3], w2[:, PASS + HALF : 2 * PASS])
        load_factor(gs_sb, gs)
        load_rows(raw[4], w4[0:PASS, 0:HALF])
        load_rows(raw[5], w4[0:PASS, HALF:N])
        load_words(w3_w, w3_words.rearrange("g p c i -> g p (c i)"))
        load_rows(raw[6], w4[PASS : 2 * PASS, 0:HALF])
        load_rows(raw[7], w4[PASS : 2 * PASS, HALF:N])
        for q in range(QUADRANTS):
            nc.sync.dma_start(
                out=w3_rows[32 * q + ROWS : 32 * q + 3 * ROWS, :].bitcast(I32),
                in_=w3_scales[:, ROWS * q : ROWS * (q + 1), :].bitcast(I32))

        w_q = [quantise("w_q0", w_bf[0][:], PASS)]
        v_w = [held("v_w%d" % k, S, U32) for k in range(2)]
        gather(v_w[0], tab_w[0], idx)
        gather(v_w[1], tab_w[1], idx)
        deal(w1_w_dealt[0][:], 2, by_group(w1_w[0]), nc.scalar.copy)
        round_half(2)

        chunks = [(g, b) for g in range(GROUPS) for b in range(BLOCKS)]
        a_banks, load_banks, y_banks, gated, diff, sine = {}, {}, {}, {}, {}, {}
        x_at, z_at, x_q, z_q = {}, {}, {}, {}

        def factor(tile, c):
            g = chunks[c][0]
            return tile[:, PACK * g : PACK * (g + 1)].unsqueeze(1).to_broadcast([P, TRIPS, PACK])

        def across(bank):
            return bank[:].rearrange("p (t j) -> p j t", t=PACK)

        def words(columns):
            return columns.rearrange("p (j t) -> p j t", t=PACK)

        def multiply_a(c):
            g, b = chunks[c]
            trips = slice(TRIPS * b, TRIPS * (b + 1))
            a_banks[c] = psum.tile([P, PASS], F32, name="a_bank%d" % c, tag="bank%d" % (BLOCKS + b))
            for k in range(2):
                for t in range(PACK):
                    first = LIFT * k + S + PASS * g + P * t
                    nc.tensor.matmul_mx(
                        out=a_banks[c][:, TRIPS * t : TRIPS * (t + 1)],
                        lhsT=w1_w_dealt[g][:, PASS * k + P * t : PASS * k + P * (t + 1)].bitcast(FP4X4),
                        lhsT_scale=planes[:, first : first + P],
                        rhs=v_w[k][:, trips].bitcast(FP8X4),
                        rhs_scale=planes[:, LIFT * k + TRIPS * b : LIFT * k + TRIPS * (b + 1)],
                        start=(k == 0 and t == 0), stop=(k == 1 and t == PACK - 1),
                    )

        def multiply_load(c):
            g, b = chunks[c]
            trips = slice(TRIPS * b, TRIPS * (b + 1))
            load_banks[c] = psum.tile([P, PASS], F32, name="load_bank%d" % c, tag="bank%d" % b)
            codes, plane = w_q[g]
            for t in range(PACK):
                nc.tensor.matmul_mx(
                    out=load_banks[c][:, TRIPS * t : TRIPS * (t + 1)],
                    lhsT=codes[:, P * t : P * (t + 1)].bitcast(FP8X4), lhsT_scale=plane[:, P * t : P * (t + 1)],
                    rhs=v2_w[:, trips].bitcast(FP4X4), rhs_scale=v2_plane[:, trips],
                    start=True, stop=True,
                )

        def gate(c):
            gated[c] = held("gated%d" % c, PASS, F32)
            nc.scalar.activation(out=words(gated[c][:]), in_=across(a_banks[c]), func=ACT.Silu)

        def subtract(c):
            diff[c] = held("diff%d" % c, PASS, F32)
            nc.vector.tensor_tensor(words(diff[c][:]), words(gated[c][:]), across(load_banks[c]), ALU.subtract)

        def take_sine(c):
            sine[c] = held("sine%d" % c, PASS, F32)
            nc.scalar.activation(out=sine[c][:], in_=diff[c][:], func=ACT.Sin)

        def make_x(c):
            nc.vector.tensor_tensor(words(x_at[c]), across(load_banks[c]), factor(gl_sb, c), ALU.mult)

        def make_z(c):
            engine = nc.gpsimd if c in GPSIMD_Z else nc.vector
            engine.tensor_tensor(words(z_at[c]), words(sine[c][:]), factor(gs_sb, c), ALU.mult)

        def operand(pair, j):
            codes, plane = pair
            return codes[:, TRIPS * j : TRIPS * (j + 1)].bitcast(FP8X4), plane[:, TRIPS * j : TRIPS * (j + 1)]

        def multiply_x(g, b):
            codes, plane = x_q[BLOCKS * g + b]
            for t in range(PACK):
                nc.tensor.matmul_mx(
                    out=y_banks[b][:, TRIPS * t : TRIPS * (t + 1)],
                    lhsT=w3_w_dealt[:, N * g + P * t : N * g + P * (t + 1)].bitcast(FP8X4),
                    lhsT_scale=w3_planes[ROWS * (g + 1) : P, P * t : P * (t + 1)],
                    rhs=codes, rhs_scale=plane, start=False, stop=False,
                )

        def multiply_z(g, b):
            if g == 0:
                y_banks[b] = psum.tile([P, PASS], F32, name="y_bank%d" % b, tag="bank%d" % (BLOCKS, BLOCKS + 1, 0, 1)[b])
            codes, plane = z_q[BLOCKS * g + b]
            w4_codes, w4_plane = w_q[2 + g]
            for t in range(PACK):
                nc.tensor.matmul_mx(
                    out=y_banks[b][:, TRIPS * t : TRIPS * (t + 1)],
                    lhsT=w4_codes[:, P * t : P * (t + 1)].bitcast(FP8X4), lhsT_scale=w4_plane[:, P * t : P * (t + 1)],
                    rhs=codes, rhs_scale=plane,
                    start=(g == 0 and t == 0), stop=(g == GROUPS - 1 and t == PACK - 1),
                )

        y = [held("y%d" % b, PACK * TRIPS, F32) for b in range(BLOCKS)]
        y_bf = held("y_bf", PACK * S, BF16)
        y_codes = held("y_codes", S, U32)
        y_plane = held("y_plane", S, U8)

        def store_y(b):
            nc.scalar.copy(out=y[b][:], in_=y_banks[b][:])
            nc.sync.dma_start(
                out=out_0.rearrange("(p t) j -> p t j", t=PACK)[:, :, TRIPS * b : TRIPS * (b + 1)],
                in_=y[b][:].rearrange("p (t j) -> p t j", t=PACK),
            )

        def round_y(b):
            nc.vector.tensor_copy(
                out=y_bf[:, PASS * b : PASS * (b + 1)].rearrange("p (c e t) -> p c t e", t=PACK, e=2),
                in_=y[b][:].rearrange("p (t c e) -> p c t e", t=PACK, e=2))

        def quantise_y(first, last):
            trips = slice(TRIPS * first, TRIPS * last)
            nc.vector.quantize_mx(
                out=y_codes[:, trips].bitcast(FP8X4), scales=y_plane[:, trips], in_=y_bf[:, PASS * first : PASS * last])

        def store_codes(first, last):
            trips = slice(TRIPS * first, TRIPS * last)
            nc.sync.dma_start(
                out=out_1[0].rearrange("p m t -> p (m t)").bitcast(I32)[:, trips], in_=y_codes[:, trips].bitcast(I32))

        x_first = held("x_first_bf", BLOCKS * PASS, BF16, "x_first")
        z_first = [held("z_first%d" % j, 2 * PASS, BF16) for j in range(2)]
        xz = [held("xz%d" % b, 2 * PASS, BF16) for b in range(BLOCKS)]
        for b in range(BLOCKS):
            x_at[b] = x_first[:, PASS * b : PASS * (b + 1)]
            z_at[b] = z_first[b // 2][:, PASS * (b % 2) : PASS * (b % 2 + 1)]
            x_at[BLOCKS + b] = xz[b][:, 0:PASS]
            z_at[BLOCKS + b] = xz[b][:, PASS : 2 * PASS]
        for c in range(BLOCKS):
            multiply_load(c)
        for c in range(BLOCKS):
            make_x(c)
        for c in range(BLOCKS):
            multiply_a(c)

        count = len(chunks)
        last = count - 1
        gate(0)
        gate(1)
        nc.gpsimd.tensor_scalar(
            w_bf[1][:].rearrange("p (t m i) -> p m t i", t=PACK, i=PACK)[:, P // 2 : P],
            raw[3][:].rearrange("p (i m t) -> p m t i", i=PACK, t=PACK), 1.0, 0.0, ALU.mult, ALU.add)
        for step in range(count + 2):
            if step < count:
                subtract(step)
                take_sine(step)
            if BLOCKS <= step < count:
                make_x(step)
            if step == 0:
                deal(w1_w_dealt[1][:], 2, by_group(w1_w[1]))
            if BLOCKS <= step + 2 < count:
                multiply_a(step + 2)
            if step + 2 < count:
                gate(step + 2)
            if step == count:
                x_q[last] = operand(quantise("x_last", x_at[last], TRIPS), 0)
            if 1 <= step <= count:
                make_z(step - 1)
            if step == 1:
                pair = quantise("x_first", x_first[:], S, "gated1")
                for b in range(BLOCKS):
                    x_q[b] = operand(pair, b)
                w_q.append(quantise("w_q1", w_bf[1][:], PASS))
            if BLOCKS <= step + 2 < count:
                multiply_load(step + 2)
            if step == 4:
                deal(w3_w_dealt[:], 4, by_group(w3_w))
            if step == 6:
                deal(w3_planes[:], 1, by_group(w3_rows))
            if 2 <= step < 6:
                round_half(step + 2, nc.vector.tensor_copy if step < 4 else nc.scalar.copy)
            if step in (4, 6):
                w_q.append(quantise("w_q%d" % (step // 2), w_bf[step // 2][:], PASS))
            if step in (3, 5):
                j = step // 2 - 1
                pair = quantise("z_first%d" % j, z_first[j][:], 2 * TRIPS)
                z_q[2 * j], z_q[2 * j + 1] = operand(pair, 0), operand(pair, 1)
            if step in (4, 5):
                for b in (2 * (step - 4), 2 * (step - 4) + 1):
                    multiply_z(0, b)
            if step == 6:
                for b in range(BLOCKS):
                    multiply_x(0, b)
            if BLOCKS <= step - 2 < last:
                pair = quantise("xz%d" % step, xz[step - 2 - BLOCKS][:], 2 * TRIPS)
                x_q[step - 2], z_q[step - 2] = operand(pair, 0), operand(pair, 1)
            if step == count + 1:
                z_q[last] = operand(quantise("z_last", z_at[last], TRIPS), 0)
            if step >= 6:
                multiply_x(1, step - 6)
                multiply_z(1, step - 6)
                store_y(step - 6)

        round_y(0)
        round_y(1)
        round_y(2)
        quantise_y(0, 2)
        quantise_y(2, 3)
        store_codes(0, 3)
        round_y(3)
        quantise_y(3, 4)
        store_codes(3, 4)

        for q in range(QUADRANTS):
            (nc.scalar if q < 3 else nc.sync).dma_start(
                out=out_2[0, ROWS * q : ROWS * (q + 1), :].bitcast(I32),
                in_=y_plane[32 * q : 32 * q + ROWS, :].bitcast(I32),
            )
